import numpy as np, ml_dtypes
CORES = [2,3,42,43,82,83,122,123]
N = 8
BF = ml_dtypes.bfloat16
L, F, M, Q, S, R, C, P = 1024, 512, 512, 4, 3, 2, 128, 8
A, ND, W = L + F, Q * M, L + F + Q * M
def pull(y, ix):
    return np.take_along_axis(y, ix[:, :, None, :], 3)
def evaluate(y, kd, om):
    for l in range(Q):
        i = l * M
        a = pull(y, kd[:, :, i:i + M]); b = pull(y, kd[:, :, ND + i:ND + i + M])
        y[..., A + i:A + i + M] = np.where(om[:, :, None, i:i + M] == 1, np.maximum(a, b), np.minimum(a + b, 255))
def begin(v, kd, om):
    y = np.zeros((N, 8, 16, W), np.int64); y[..., :A] = v
    evaluate(y, kd, om)
    return y
def values(rng, lo, hi):
    return (rng.random((N, 8, 16, A)) * np.exp2(rng.integers(lo, hi + 1, (N, 8, 1, A)))).astype(np.int64)
def kids(rng, near, other):
    k = np.zeros((N, 8, 2, Q, M), np.int64); sh = (N, 8, 2, M)
    for l in range(Q):
        c = rng.random(sh)
        x = rng.integers(A + max(l - 1, 0) * M, A + max(l, 1) * M, sh); z = rng.integers(0, A + l * M, sh); e = rng.integers(0, A, sh)
        k[:, :, :, l] = np.where((c < near) & (l > 0), x, np.where(c < near + other, z, e))
    return k
def aims(rng, v, k, o, share):
    y = begin(v, k.reshape(N, 8, 2 * ND), o)[..., W - M:]
    e = rng.random((N, 8, 1, M)); close = np.clip(y + rng.integers(-20, 21, y.shape), 0, 255)
    far = (rng.random(y.shape) * np.exp2(rng.integers(4, 9, (N, 8, 1, M)))).astype(np.int64)
    return np.where(e < share, y, np.where(e < share + (1 - share) * 0.5, close, far))
def ops(rng, share):
    return (rng.random((N, 8, ND)) < share).astype(np.int64)
def weights(rng, share):
    return (rng.random((N, 8, 16, 2)) < share).astype(np.int64)
def pack(v, k, o, g, w):
    return {"lv": np.ascontiguousarray(v.reshape(N, 128, A)).astype(np.float32).astype(BF), "kid": np.ascontiguousarray(k.reshape(N, 8, 2 * ND)).astype(np.int32),
            "mx": np.ascontiguousarray(o).astype(np.int32), "tg": np.ascontiguousarray(g.reshape(N, 128, M)).astype(np.float32).astype(BF),
            "wt": np.ascontiguousarray(w.reshape(N, 128, 2)).astype(np.int32)}
def setup_inputs(rng):
    v = values(rng, 4, 8); k = kids(rng, 0.5, 0.25); o = ops(rng, 0.4)
    return pack(v, k, o, aims(rng, v, k, o, rng.choice(np.array([0.2, 0.5, 0.8, 0.97]), (N, 8, 1, 1))), weights(rng, 0.6))
def setup_inputs_room(rng):
    v = rng.integers(1, 128, (N, 8, 16, A)); v[..., L:L + 2] = 0; v[:, :, 0, L + 1] = 1
    k = kids(rng, 0.5, 0.25); o = ops(rng, 0.4); w = weights(rng, 0.6)
    k[:, :, :, Q - 1] = rng.integers(0, A, (N, 8, 2, M)); o[:, :, ND - M:] = 0
    g = pull(v, k[:, :, 0, Q - 1]) + pull(v, k[:, :, 1, Q - 1])
    for q in range(N):
        for j in range(8):
            n = int(rng.choice(np.array([0, 1, C - 1, C, C + 1, M])))
            if q == 0: n = (C, C + 1, M, C - 1, 1, 0, C, C + 1)[j]
            at = np.arange(M - n, M) if q == 0 and j < 4 else rng.permutation(M)[:n]
            k[q, j, :, Q - 1, at] = L; g[q, j, :, at] = rng.integers(128, 256, (n, 16))
    k[0, 0:4:3, 1, Q - 1, M - 1] = L + 1; o[0, 0:4:3, ND - 1] = 1
    return pack(v, k, o, g, w)
def setup_inputs_ties(rng):
    few = np.array([0, 1, 2, 127, 128, 254, 255]); pal = rng.choice(few, (N, 8, 16, 6)).astype(np.int64)
    v = pull(pal, rng.integers(0, 6, (N, 8, A))); k = kids(rng, 0.4, 0.2)
    k[:, :, 1] = np.where(rng.random((N, 8, Q, M)) < 0.3, k[:, :, 0], k[:, :, 1])
    g = np.where(rng.random((N, 8, 1, M)) < 0.5, pull(pal, rng.integers(0, 6, (N, 8, M))), rng.choice(few, (N, 8, 16, M)))
    return pack(v, k, ops(rng, 0.5), g, weights(rng, 0.5))
def setup_inputs_meet(rng):
    v = values(rng, 3, 6); k = kids(rng, 0.5, 0.25)
    for l in range(1, Q):
        some = rng.integers(0, M, (N, 8, 8))
        k[:, :, :, l] = A + (l - 1) * M + np.take_along_axis(some, rng.integers(0, 8, (N, 8, 2 * M)), 2).reshape(N, 8, 2, M)
    k[:, 1::2, :, Q - 1] = k[:, 1::2, :, Q - 1, :1]
    return pack(v, k, ops(rng, 0.7), rng.integers(0, 256, (N, 8, 16, M)), weights(rng, 0.6))
def setup_inputs_ends(rng):
    v = np.where(rng.random((N, 8, 16, A)) < rng.random((N, 8, 1, A)), 255, 0)
    k = kids(rng, 1.0, 0.0); o = ops(rng, 0.5); w = weights(rng, 0.6); w[:, 0::4] = 1; w[:, 1::4] = 0
    for l in range(Q):
        c = [0, L - 1, L, A - 1] + ([A, A + (l - 1) * M, A + l * M - 1] if l else [])
        k[:, 0::2, :, l] = rng.choice(np.array(c), (N, 4, 2, M))
    g = np.where(rng.random((N, 8, 16, M)) < rng.random((N, 8, 1, M)), 255, 0)
    g[..., 0] = 255; g[..., M - 1] = 255; g[..., 1] = 0
    o[..., ND - M] = 1
    for j in (0, 4, 6):
        k[:, j, :, Q - 1, 0] = 0; v[:, j, :, 0] = 0; v[:, j, 0, 1:L] = 255
    w[:, 4] = 1; w[:, 4, 15, 0] = 0; g[:, 4, 15, 0] = 111
    w[:, 6] = 1; w[:, 6, 15, 0] = 0; v[:, 6, :, 1:L] = rng.integers(0, 5, (N, 16, L - 1)); v[:, 6, 0, 1:L] = rng.integers(1, 5, (N, L - 1))
    return pack(v, k, o, g, w)
def setup_inputs_spread(rng):
    v = (rng.random((N, 8, 16, A)) * np.exp2(8 * rng.random((N, 8, 1, A)))).astype(np.int64) * (rng.random((N, 8, 1, A)) > 0.0625)
    near = rng.random((N, 8, 1, 1)); k = kids(rng, near, (1 - near) * rng.random((N, 8, 1, 1))); o = ops(rng, rng.random((N, 8, 1)))
    return pack(v, k, o, aims(rng, v, k, o, rng.random((N, 8, 1, 1))), weights(rng, rng.random((N, 8, 1, 2))))
def check_inputs(d):
    bad = []
    for nm in ("lv", "tg"):
        x = d[nm].astype(np.float32)
        if not (np.min(x) >= 0 and np.max(x) <= 255): bad.append("range of " + nm)
        if np.any(x != np.floor(x)): bad.append("whole numbers in " + nm)
    for nm in ("mx", "wt"):
        if np.min(d[nm]) < 0 or np.max(d[nm]) > 1: bad.append("range of " + nm)
    k = d["kid"].reshape(N, 8, 2, Q, M)
    for l in range(Q):
        if np.min(k[:, :, :, l]) < 0 or np.max(k[:, :, :, l]) >= A + l * M: bad.append("range of kid in level " + str(l))
    return bad
def reference(lv, kid, mx, tg, wt):
    kd = kid.astype(np.int64); om = mx.astype(np.int64)
    y = begin(lv.astype(np.float32).astype(np.int64).reshape(N, 8, 16, A), kd, om)
    goal = tg.astype(np.float32).astype(np.int64).reshape(N, 8, 16, M); w = wt.astype(np.int64).reshape(N, 8, 16, 2)
    for rnd in range(R):
        node = np.tile(ND - M + np.arange(M), (N, 8, 1)); live = np.ones((N, 8, M), bool); want = goal
        par = np.zeros((N, 8, M), np.int64); side = np.zeros((N, 8, M), np.int64); child = np.zeros((N, 8, M), np.int64); err = np.zeros((N, 8, M), np.int64)
        for step in range(S):
            ka = np.take_along_axis(kd, node, 2); kb = np.take_along_axis(kd, node + ND, 2); o = np.take_along_axis(om, node, 2)[:, :, None, :] == 1
            ya = pull(y, ka); yb = pull(y, kb)
            wa = np.where(o, np.where(want >= yb, want, 0), np.maximum(want - yb, 0))
            wb = np.where(o, np.where(want >= ya, want, 0), np.maximum(want - ya, 0))
            ea = np.add.reduce(np.abs(wa - ya), axis=2); eb = np.add.reduce(np.abs(wb - yb), axis=2)
            tob = eb < ea
            par = np.where(live, node, par); side = np.where(live, tob, side); child = np.where(live, np.where(tob, kb, ka), child); err = np.where(live, np.where(tob, eb, ea), err)
            want = np.where(live[:, :, None, :], np.where(tob[:, :, None, :], wb, wa), want)
            live = live & (child >= A); node = np.where(live, child - A, 0)
        u1 = np.add.reduce(w[..., 0:1] * want, axis=2); u2 = np.add.reduce(w[..., 1:2] * want, axis=2)
        h = ((u1 * u2) >> 5) + u2; stride = 2 * (u1 & 127) + 1
        cand = (h[:, :, None, :] + np.arange(P)[None, None, :, None] * stride[:, :, None, :]) & (L - 1)
        off = np.abs(pull(y, cand.reshape(N, 8, P * M)).reshape(N, 8, 16, P, M) - want[:, :, :, None, :])
        ce = np.add.reduce(off, axis=2); m = np.argmin(ce, axis=2)
        donor = np.take_along_axis(cand, m[:, :, None, :], 2)[:, :, 0]
        hit = np.min(ce, axis=2) < err; one = hit.astype(np.int64)
        counts = hit & (np.add.accumulate(one, axis=2) - one < C)
        go = {}
        for q in range(N):
            for g in range(8):
                i = np.flatnonzero(counts[q, g]); go[q, g] = y[q, g][:, child[q, g, i]]
                key, first = np.unique(side[q, g, i] * ND + par[q, g, i], return_index=True)
                kd[q, g, key] = donor[q, g, i[first]]
        for q in range(N):
            for g in range(8):
                v = go[q, g]; y[(q + 1) % N, g, :, rnd * C:rnd * C + v.shape[1]] = v
        evaluate(y, kd, om)
    return {"yo": y.reshape(N, 128, W).astype(np.float32).astype(BF), "ko": kd.astype(np.float32)}

@@ -1,0 +1,595 @@
+from concourse.mybir import AluOpType as A, ActivationFunctionType as F
+
+H = 16
+LIB = 1024
+SENT = -1048576.0
+
+SCRATCH, PLACE = {}, {}
+
+
+def declare(dtype, text, packed=False):
+    o = 0
+    for item in text.split():
+        name, w = item.split(":")
+        if packed:
+            PLACE[name] = ("SM" + dtype, o)
+            o += (int(w) + 7) // 8 * 8
+        else:
+            SCRATCH[name] = ("sbuf", [128, int(w)], dtype)
+    if packed:
+        SCRATCH["SM" + dtype] = ("sbuf", [128, o], dtype)
+
+
+declare("bfloat16", "YT:3616 YAB:4096 NWB:128 NW3:32 TG:512 WAB0:1536 WAB1:1536 Y2:1024 SB:1024 NY:1024 AB:1024 BP:512 WT:512 MT:512 DF:4096 GV:1024 "
+        "YC:512 LF:128 LT2:128 HIT:32 INC:32 EQ:1024 QH:1024 ONE:128 IB:128 NI:128 BD:128 BD1:128 O256:2048 BQ:2048 KQ0:2048 KQ1:2048 KQ2:2048 MQ:2048 "
+        "W1:2048 W2:2048 AQ:2048 BQ2:128 LB:128 LT:128 TRI:128 I5:128 IO1:128 IOC:256 MCI:256 MC:256")
+declare("float16", "KLH:256 MLH:128 WF:256 KTG:512 XH:32 DNH:32 DG:1024 CHM:2048 IH:128")
+declare("uint16", "UL:384 SEL:32 NL:32 KEYU:32 CU:256 SLOT:32")
+declare("int32", "KLD:256 MLD:128 WTI:2")
+declare("float32", "KT:1536 PAY:512 SL0:640 SL1:640 LAND0:128 LAND1:128 KOF:256 WTF:2")
+declare("float32", "WK:256 NW:128 NKB:128 ES:64 TOB:32 DK:32 QC:32 Q0:32 Q1:32 S1:32 S2:32 S3:32 CHI:32 ST:64 NS:64 DS:64 LV:64 NB:32 XG:32 US:64 B1:128 B2:64 "
+        "B3:64 BEST:32 CT:32 RD:32 RE:32 RF:32 XF:16 DX:8 XN:8 XK:8 QF:8 CF:8 WIN:8 DD:8 ZU:256 ZT:256 STR:32 SR2:64 SR4:128 SELC:16 LANE:32 LQ:32 LQ2:32 "
+        "TC:32 TM:32 G16:8", True)
+declare("int32", "LI:128 LY:128 U1I:32 PRI:32 SHI:32 UMI:32 CA:256 CI:256 B8:32 MI:32 MTT:32 HD:32 DNI:32 XI:16 XS:16 KI:8 QI:8 CQ:8 KPI:32 KAI:32 KBI:32 "
+        "LI0:32 LI1:32 LI2:32", True)
+for _k in range(8):
+    SCRATCH["P%d" % _k] = ("psum", [128, 512], "float32")
+
+SEMAPHORES = ["cV", "cS", "cP", "cG", "arr0", "arr1", "snt0", "snt1"] + ["d%d" % k for k in range(16)]
+
+
+def rank_program(g, core, T, topo):
+    rank = T.rank_of(core)
+    if rank is None:
+        return
+    n_ranks = len(T.cores)
+    ENG = {"V": g.vector, "S": g.scalar, "P": g.tensor, "G": g, "Y": g.sync}
+    cnt = {s: 0 for s in SEMAPHORES}
+    seen = {q: {} for q in ENG}
+    clocks = {}
+    acc = {}
+    dmas = [0]
+
+    def ap(r):
+        if r[0] == "ind":
+            return ap(r[1]).indirect(ap(r[2]))
+        b, lo, hi, st, p0, p1 = r
+        if b in PLACE:
+            b, o = PLACE[b]
+            lo, hi = lo + o, hi + o
+        return T[b][p0:p1, lo:hi] if st == 1 else T[b][p0:p1, lo:hi:st]
+
+    def R(b, lo, hi, st=1, p0=0, p1=128):
+        return (b, lo, hi, st, p0, p1)
+
+    def is_psum(b):
+        return b[0] == "P" and len(b) == 2
+
+    def wait(q, sem, n):
+        if seen[q].get(sem, 0) >= n:
+            return
+        ENG[q].wait_ge(T.sem[sem], n)
+        s = seen[q]
+        for k, v in list(clocks.get((sem, n), {}).items()) + [(sem, n)]:
+            s[k] = max(s.get(k, 0), v)
+
+    def sync_for(q, reads, writes):
+        need = {}
+        for rs, w in ((reads, False), (writes, True)):
+            for (b, lo, hi, st, p0, p1) in rs:
+                ps = is_psum(b)
+                if ps:
+                    lo, hi, p0, p1 = 0, 512, 0, 128
+                for (q2, sem, n, lo2, hi2, a0, a1, w2) in acc.get(b, ()):
+                    if lo2 >= hi or hi2 <= lo or a0 >= p1 or a1 <= p0:
+                        continue
+                    if ps and q2 == q and (q == "P" or not (w or w2)):
+                        continue
+                    if not ps and not (w or w2):
+                        continue
+                    need[sem] = max(need.get(sem, 0), cnt[sem] if sem[0] == "d" else n)
+        for sem in sorted(need, key=lambda s: -sum(clocks.get((s, need[s]), {}).values())):
+            wait(q, sem, need[sem])
+
+    def note(q, sem, n, reads, writes):
+        for rs, w in ((writes, True), (reads, False)):
+            for (b, lo, hi, st, p0, p1) in rs:
+                if is_psum(b):
+                    lo, hi, p0, p1 = 0, 512, 0, 128
+                L = acc.setdefault(b, [])
+                if w and st == 1:
+                    L[:] = [e for e in L if not (lo <= e[3] and e[4] <= hi and p0 <= e[5] and e[6] <= p1)]
+                elif not w:
+                    L[:] = [e for e in L if not (e[0] == q and not e[7] and lo <= e[3] and e[4] <= hi and p0 <= e[5] and e[6] <= p1)]
+                L.append((q, sem, n, lo, hi, p0, p1, w))
+
+    def emit(q, fn, reads, writes):
+        sync_for(q, reads, writes)
+        sem = "c" + q
+        cnt[sem] += 1
+        fn().then_inc(T.sem[sem], 1)
+        clocks[(sem, cnt[sem])] = dict(seen[q], **{sem: cnt[sem]})
+        note(q, sem, cnt[sem], reads, writes)
+
+    def newd():
+        dmas[0] += 1
+        return "d%d" % (dmas[0] - 1)
+
+    def dma(q, sem, out, in_, reads, writes):
+        sync_for(q, reads, writes)
+        cnt[sem] += 16
+        ENG[q].dma_start(out, in_).then_inc(T.sem[sem], 16)
+        c = dict(seen[q])
+        for k, v in clocks.get((sem, cnt[sem] - 16), {}).items():
+            c[k] = max(c.get(k, 0), v)
+        clocks[(sem, cnt[sem])] = c
+        note(q, sem, cnt[sem], reads, writes)
+
+    def IND(win, off):
+        return ("ind", win, off)
+
+    def rd(*xs):
+        r = []
+        for x in xs:
+            if isinstance(x, tuple):
+                r += [x[1], x[2]] if x[0] == "ind" else [x]
+        return r
+
+    def num(x):
+        return ap(x) if isinstance(x, tuple) else x
+
+    def tt(out, a, b, op):
+        emit("V", lambda: g.vector.tensor_tensor(ap(out), ap(a), ap(b), op), rd(a, b), [out])
+
+    def ts(out, a, s1, op0, s2=None, op1=None):
+        if op1 is None:
+            emit("V", lambda: g.vector.tensor_scalar(ap(out), ap(a), num(s1), None, op0), rd(a, s1), [out])
+        else:
+            emit("V", lambda: g.vector.tensor_scalar(ap(out), ap(a), num(s1), num(s2), op0, op1), rd(a, s1, s2), [out])
+
+    def cp(out, a):
+        if out[0] == "ind":
+            emit("V", lambda: g.vector.tensor_copy(ap(out), ap(a)), rd(a) + [out[2]], [out[1]])
+        else:
+            emit("V", lambda: g.vector.tensor_copy(ap(out), ap(a)), rd(a), [out])
+
+    def ms(out, v):
+        emit("V", lambda: g.vector.memset(ap(out), v), [], [out])
+
+    def act(out, a, func=F.Identity, scale=1.0):
+        emit("S", lambda: g.scalar.activation(ap(out), ap(a), func, bias=0.0, scale=num(scale)), rd(a, scale), [out])
+
+    def mm(out, lhsT, rhs, start, stop):
+        emit("P", lambda: g.tensor.matmul(ap(out), ap(lhsT), ap(rhs), start, stop), [lhsT, rhs], [out])
+
+    def iota(out, pat, chm, small):
+        if small:
+            emit("G", lambda: g.iota(ap(out), pat, 0, chm, allow_small_or_imprecise_dtypes=True), [], [out])
+        else:
+            emit("G", lambda: g.iota(ap(out), pat, 0, chm), [], [out])
+
+    def asel(out, in_, pat, op, base, chm):
+        emit("G", lambda: g.affine_select(ap(out), ap(in_), pat, op, 0.0, base, chm), [in_], [out])
+
+    def phases(out_b, lo, n, W, src, s0, first, last):
+        for q in range(16):
+            mm(R(out_b, lo, lo + n), R(W, 128 * q, 128 * q + 128), R(src, s0 + q, s0 + 16 * n, 16), first and q == 0, last and q == 15)
+
+    def to_rows(P, W, src):
+        for q in range(16):
+            yield R(P, q, 512, 16), R(W, 128 * q, 128 * q + 128), src
+
+    a128 = lambda b: R(b, 0, 128)
+    c32 = lambda b, k=0: R(b, 32 * k, 32 * k + 32)
+
+    dK0, dK1, dM, dL, dT, dW = [newd() for _ in range(6)]
+
+    def load_kids(q, sem, s, l0, l1):
+        for gr in range(8):
+            dst = R("KLD", s * 128 + 16 * gr, s * 128 + 16 * gr + 16, 1, 32 * l0, 32 * l1)
+            dma(q, sem, ap(dst), T.kid[gr:gr + 1, s * 2048 + 512 * l0:s * 2048 + 512 * l1], [], [dst])
+    load_kids("Y", dK0, 0, 0, 1)
+    load_kids("S", dK0, 1, 0, 1)
+    dma("Y", dL, ap(R("YT", H, H + 1536)), T.lv[:, :], [], [R("YT", H, H + 1536)])
+    for gr in range(8):
+        dst = R("MLD", 16 * gr, 16 * gr + 16)
+        dma("S", dM, ap(dst), T.mx[gr:gr + 1, :], [], [dst])
+    load_kids("Y", dK1, 0, 1, 4)
+    load_kids("S", dK1, 1, 1, 4)
+    dma("Y", dT, ap(R("TG", 0, 512)), T.tg[:, :], [], [R("TG", 0, 512)])
+    dma("Y", dW, ap(R("WTI", 0, 2)), T.wt[:, :], [], [R("WTI", 0, 2)])
+
+    ms(a128("ONE"), 1.0)
+    ms(R("YT", 0, H), 0.0)
+    ms(R("O256", 0, 2048), 256.0)
+    ms(R("MQ", 0, 2048), 0.0)
+    asel(a128("IB"), a128("ONE"), [[-1, 128]], A.is_equal, 0, 1)
+    asel(a128("BD1"), a128("ONE"), [[-16, 8], [0, 16]], A.is_ge, 0, 1)
+    asel(a128("BD"), a128("BD1"), [[16, 8], [0, 16]], A.is_ge, 15, -1)
+    iota(R("LI0", 0, 32), [[16, 32]], 0, False)
+    iota(R("LI1", 0, 32), [[0, 32]], 1, False)
+    asel(R("BQ", 0, 2048), R("O256", 0, 2048), [[-1, 16], [-16, 8], [0, 16]], A.is_equal, 0, 1)
+    for k in range(3):
+        asel(R("KQ%d" % k, 0, 2048), R("BQ", 0, 2048), [[0, 16], [0, 8], [1, 16]], A.is_equal, -k, 0)
+    asel(a128("LT"), a128("BD"), [[1, 128]], A.is_gt, 0, -1)
+    asel(a128("TRI"), a128("ONE"), [[-1, 128]], A.is_gt, 0, 1)
+    iota(R("MCI", 0, 256), [[1, 8], [0, 32]], 0, True)
+    iota(R("IO1", 0, 128), [[1, 128]], 0, True)
+    iota(R("IOC", 0, 256), [[32, 4], [128, 2], [1, 32]], 0, True)
+    iota(R("G16", 0, 8), [[16, 8]], 0, True)
+    cp(a128("IH"), a128("IB"))
+    ts(a128("NI"), a128("IB"), -1.0, A.mult)
+    for gr in range(8):
+        cp(R("MQ", 16 * gr, 2048, 129), R("BD", 16 * gr, 16 * gr + 16))
+    ts(c32("LI2"), c32("LI1"), 15, A.bitwise_and)
+    ts(c32("Q0"), c32("LI2"), 0.0, A.is_equal)
+    ts(c32("Q1"), c32("LI2"), 1.0, A.is_equal, 4096.0, A.mult)
+    tt(c32("QC"), c32("Q0"), c32("Q1"), A.add)
+    act(R("AQ", 0, 2048), R("MQ", 0, 2048), scale=R("QC", 0, 1))
+
+    def constants_1():
+        cp(R("WTF", 0, 2), R("WTI", 0, 2))
+        ts(R("W1", 0, 2048), R("MQ", 0, 2048), R("WTF", 0, 1), A.mult)
+        ts(R("W2", 0, 2048), R("MQ", 0, 2048), R("WTF", 1, 2), A.mult)
+
+    def constants_2():
+        ts(c32("TC"), c32("LANE"), 128.0, A.add)
+        ts(c32("TM"), c32("LANE"), -383.0, A.add)
+        ts(R("MC", 0, 256), R("MCI", 0, 256), 0.125, A.mult)
+        for s in range(2):
+            ts(R("SELC", 8 * s, 8 * s + 8), R("BQ", 128 * s, 128 * s + 128, 16), 1.0 / 256, A.mult)
+        ts(a128("I5"), a128("IB"), -512.0, A.mult)
+        tt(a128("LB"), a128("LT"), a128("BD"), A.subtract)
+        tt(a128("LB"), a128("LB"), a128("IB"), A.add)
+        tt(a128("LT"), a128("LB"), a128("I5"), A.add)
+
+    def load_level(l):
+        P = "P%d" % (7 - l)
+        for s in range(2):
+            ts(R("KLH", s * 128, s * 128 + 128, 1, 32 * l, 32 * l + 32), R("KLD", s * 128, s * 128 + 128, 1, 32 * l, 32 * l + 32), -1792.0, A.add)
+        ts(R("MLH", 0, 128, 1, 32 * l, 32 * l + 32), R("MLD", 0, 128, 1, 32 * l, 32 * l + 32), -1.0, A.mult, 1.0, A.add)
+        idr = R("IH", 32 * l, 32 * l + 32, 1, 32 * l, 32 * l + 32)
+        for s in range(2):
+            mm(R(P, 32 * s, 32 * s + 32), R("KLH", s * 128, s * 128 + 128, 1, 32 * l, 32 * l + 32), idr, True, True)
+        mm(R(P, 64, 96), R("MLH", 0, 128, 1, 32 * l, 32 * l + 32), idr, True, True)
+        ts(R("WK", 64 * l, 64 * l + 64), R(P, 0, 64), 1792.0 + H, A.add)
+        cp(c32("NW", l), R(P, 64, 96))
+
+    def lists(l):
+        tt(c32("NKB", l), R("WK", 64 * l + 32, 64 * l + 64), c32("NW", l), A.mult)
+        cp(R("UL", 96 * l + 64, 96 * l + 96), c32("NKB", l))
+        cp(R("UL", 96 * l, 96 * l + 64), R("WK", 64 * l, 64 * l + 64))
+
+    def level(l, last, between=None):
+        W = R("YT", 0, H + 1536 + 512 * l)
+        cut = ((0, 8), (8, 32))
+        for a, b in cut:
+            act(R("BP", 16 * a, 16 * b), IND(W, R("UL", 96 * l + 64 + a, 96 * l + 64 + b)))
+        if between:
+            between()
+        for a, b in cut:
+            c = (16 * a, 16 * b)
+            tt(R("WT", *c), IND(W, R("UL", 96 * l + a, 96 * l + b)), R("BP", *c), A.add)
+            tt(R("MT", *c), IND(W, R("UL", 96 * l + 32 + a, 96 * l + 32 + b)), R("WT", *c), A.max)
+            o = H + 1536 + 512 * l
+            ts(R("YT", o + c[0], o + c[1]), R("MT", *c), 255.0, A.min)
+        if not last:
+            act(R("YAB", 2048 + 512 * l, 2560 + 512 * l), IND(W, R("UL", 96 * l + 32, 96 * l + 64)))
+            if l < 3:
+                act(R("YAB", 512 * l, 512 * l + 512), IND(W, R("UL", 96 * l, 96 * l + 32)))
+            else:
+                cp(R("YAB", 512 * l, 512 * l + 512), IND(W, R("UL", 96 * l, 96 * l + 32)))
+
+    def wf(ls):
+        for l in ls:
+            for s in range(2):
+                ts(R("WF", 128 * s + 32 * l, 128 * s + 32 * l + 32), R("WK", 64 * l + 32 * s, 64 * l + 32 * s + 32), -1792.0 - H, A.add)
+
+    def kt(l):
+        P = "P%d" % (7 - l)
+        srcs = (R("WF", 32 * l, 32 * l + 32), R("WF", 128 + 32 * l, 160 + 32 * l), c32("NWB", l))
+        for q in range(16):
+            for k in range(3):
+                mm(R(P, q, 512, 16), R("KQ%d" % k, 128 * q, 128 * q + 128), srcs[k], k == 0, k == 2)
+
+    def kt_copy():
+        for l in range(3):
+            act(R("KT", 512 * l, 512 * l + 512), R("P%d" % (7 - l), 0, 512), scale=1.0 / 256)
+
+    def step(st, fill):
+        Wc, Wn = "WAB%d" % (st % 2), "WAB%d" % ((st + 1) % 2)
+        if st == 0:
+            D = R("TG", 0, 512)
+            y = (R("YAB", 1536, 2048), R("YAB", 3584, 4096))
+            ka, kb = R("WK", 192, 224), R("WK", 224, 256)
+        else:
+            D = R(Wc, 1024, 1536)
+            y = (R("Y2", 0, 512), R("Y2", 512, 1024))
+            cp(y[1], IND(R("YAB", 2048, 3584), c32("NL")))
+            act(R("KTG", 0, 512), IND(R("KT", 0, 1536), c32("NL")))
+            act(y[0], IND(R("YAB", 0, 1536), c32("NL")))
+            ka, kb = c32("KAI"), c32("KBI")
+        mm(R("P0", 0, 512), a128("IB"), D, True, True)
+        for s in range(2):
+            mm(R("P%d" % (2 + s), 0, 512), a128("IB"), D, True, False)
+        if st == 0:
+            for o, w, x in to_rows("P1", "BQ", c32("NW3")):
+                mm(o, w, x, True, True)
+            ts(c32("NB"), c32("LANE"), 1536.0, A.add)
+        else:
+            mm(R("P1", 0, 512), a128("BQ2"), R("KTG", 0, 512), True, True)
+            phases("P7", 0, 32, "AQ", "KTG", 0, True, True)
+        parts = ((0, 0, 512, "P4"), (1, 0, 256, "P5"), (1, 256, 512, "P0"))
+        for s in range(2):
+            c = (512 * s, 512 * s + 512)
+            tt(R("SB", *c), y[1 - s], R("P0", 0, 512), A.is_le)
+            tt(R("NY", *c), R("P1", 0, 512), y[1 - s], A.mult)
+            mm(R("P%d" % (2 + s), 0, 512), a128("NI"), R("NY", *c), False, True)
+        for s, a, b, P in parts:
+            mm(R(P, 0, b - a), a128("NI"), R(y[s][0], y[s][1] + a, y[s][1] + b), True, False)
+        for s, a, b, P in parts:
+            c = (512 * s + a, 512 * s + b)
+            tt(R(Wc, *c), R("SB", *c), R("P%d" % (2 + s), a, b), A.mult)
+            mm(R(P, 0, b - a), a128("IB"), R(Wc, *c), False, True)
+            act(R("AB", *c), R(P, 0, b - a), F.Abs)
+        if st:
+            ts(c32("KPI"), c32("P7"), (1792.0 + H) * 4097.0, A.add)
+            ts(c32("KAI"), c32("KPI"), 4095, A.bitwise_and)
+            ts(c32("KBI"), c32("KPI"), 12, A.arith_shift_right)
+        tt(c32("DK"), kb, ka, A.subtract)
+        fill()
+        phases("P6", 0, 64, "MQ", "AB", 0, True, True)
+        cp(R("ES", 0, 64), R("P6", 0, 64))
+        tt(c32("TOB"), c32("ES", 1), c32("ES"), A.is_lt)
+        if st == 0:
+            tt(c32("S1"), c32("TOB"), c32("LQ"), A.add)
+        else:
+            ts(c32("S1"), c32("TOB"), -2.0, A.add)
+            tt(c32("S3"), c32("S1"), c32("LV"), A.mult)
+            tt(c32("S1"), c32("S3"), c32("LQ2"), A.add)
+        if st < 2:
+            tt(c32("S2"), c32("TOB"), c32("DK"), A.mult)
+        ts(c32("SEL"), c32("S1"), 512.0, A.mult)
+        win = R(Wc, 0, 1024 if st == 0 else 1536)
+        if st < 2:
+            act(R(Wn, 1024, 1536), IND(win, c32("SEL")))
+            tt(c32("CHI"), c32("S2"), ka, A.add)
+            ts(c32("NL"), c32("CHI"), -1536.0 - H, A.add, 0.0, A.max)
+        else:
+            act(R(Wn, 1024, 1280), IND(win, R("SEL", 0, 16)))
+            cp(R(Wn, 1280, 1536), IND(win, R("SEL", 16, 32)))
+
+        def rest():
+            X = "ST" if st == 0 else "NS"
+            ts(c32("S3"), c32("TOB"), 2048.0, A.mult)
+            tt(c32(X, 1), c32("ES", 1), c32("ES"), A.min)
+            tt(c32(X), c32("S3"), c32("NB"), A.add)
+            if st:
+                tt(R("DS", 0, 64), R("NS", 0, 64), R("ST", 0, 64), A.subtract)
+                tt(R("DS", 0, 64), R("DS", 0, 64), R("LV", 0, 64), A.mult)
+                tt(R("ST", 0, 64), R("DS", 0, 64), R("ST", 0, 64), A.add)
+            if st == 0:
+                for k in range(2):
+                    ts(c32("LV", k), c32("CHI"), 1536.0 + H, A.is_ge)
+            elif st == 1:
+                ts(c32("S3"), c32("CHI"), 1536.0 + H, A.is_ge)
+                for k in range(2):
+                    tt(c32("LV", k), c32("LV", k), c32("S3"), A.mult)
+            if st < 2:
+                ts(c32("NB"), c32("CHI"), -1536.0 - H, A.add, 0.0, A.max)
+        return rest
+
+    def donors(t, rest):
+        D = R("WAB1", 1024, 1536)
+        SL = "SL%d" % t
+        phases("P6", 0, 32, "W1", "WAB1", 1024, True, True)
+        phases("P6", 32, 32, "W2", "WAB1", 1024, True, True)
+        rest()
+        cp(c32("KEYU"), c32("ST"))
+        act(R("YC", 0, 512), IND(R("YAB", 0, 4096), c32("KEYU")))
+        ts(c32("XG"), c32("ST"), 2048.0, A.is_ge)
+        tt(c32("S3"), c32("XG"), c32("ST"), A.add)
+        ts(c32("XH"), c32("S3"), -2048.0, A.add)
+        ms(R(SL, 0, 128), SENT)
+        cp(R("US", 0, 64), R("P6", 0, 64))
+        cp(c32("U1I"), c32("US"))
+        tt(c32("PRI"), c32("US"), c32("US", 1), A.mult)
+        ts(c32("UMI"), c32("U1I"), 127, A.bitwise_and)
+        ts(c32("SHI"), c32("PRI"), 5, A.arith_shift_right)
+        ts(c32("STR"), c32("UMI"), 2.0, A.mult, 1.0, A.add)
+        for k in range(4):
+            act(c32("SR4", k), c32("STR"), scale=4.0)
+        tt(c32("CA"), c32("SHI"), c32("US", 1), A.add)
+        for k in range(2):
+            ts(c32("SR2", k), c32("UMI"), 4.0, A.mult, 2.0, A.add)
+        tt(c32("CA", 1), c32("CA"), c32("STR"), A.add)
+        tt(R("CA", 64, 128), R("CA", 0, 64), R("SR2", 0, 64), A.add)
+        ts(R("CI", 0, 128), R("CA", 0, 128), 1023, A.bitwise_and)
+        cp(R("CU", 0, 128), R("CI", 0, 128))
+        LW = R("YT", H, H + LIB)
+        for k, m in enumerate((1, 3)):
+            act(R("GV", 512 * k, 512 * k + 512), IND(LW, c32("CU", m)))
+            mm(R("P%d" % (4 + 3 * k), 0, 512), a128("IB"), R("GV", 512 * k, 512 * k + 512), True, False)
+            mm(R("P%d" % (4 + 3 * k), 0, 512), a128("NI"), D, False, True)
+        for h in range(2):
+            mm(R("P%d" % (2 + h), 0, 128), a128("IB"), R("MC", 128 * h, 128 * h + 128), True, False)
+
+        def cand(m):
+            c = (512 * m, 512 * m + 512)
+            if m in (1, 3):
+                act(R("DF", *c), R("P4" if m == 1 else "P7", 0, 512), F.Abs)
+            else:
+                tt(R("DF", *c), IND(LW, c32("CU", m)), D, A.subtract)
+                act(R("DF", *c), R("DF", *c), F.Abs)
+        cand(0)
+        cand(1)
+        tt(R("CA", 128, 256), R("CA", 0, 128), R("SR4", 0, 128), A.add)
+        cand(2)
+        ts(R("CI", 128, 256), R("CA", 128, 256), 1023, A.bitwise_and)
+        cp(R("CU", 128, 256), R("CI", 128, 256))
+        cand(3)
+        phases("P2", 0, 64, "MQ", "DF", 0, False, False)
+        phases("P2", 64, 64, "MQ", "DF", 1024, False, True)
+        mm(R("P5", 0, 512), a128("IB"), R("YC", 0, 512), True, False)
+        for o, w, x in to_rows("P5", "KQ0", c32("XH")):
+            mm(o, w, x, False, False)
+        cand(4)
+        cand(5)
+        phases("P3", 0, 64, "MQ", "DF", 2048, False, False)
+        cand(6)
+        cp(R("B1", 0, 128), R("P2", 0, 128))
+        cand(7)
+        tt(R("B3", 0, 64), R("B1", 0, 64), R("B1", 64, 128), A.min)
+        phases("P3", 64, 64, "MQ", "DF", 3072, False, True)
+        tt(R("B2", 0, 64), R("B3", 0, 64), R("P3", 0, 64), A.min)
+        tt(R("B1", 0, 64), R("B2", 0, 64), R("P3", 64, 128), A.min)
+        tt(c32("BEST"), c32("B1"), c32("B1", 1), A.min)
+        ts(c32("B8"), c32("BEST"), 8.0, A.mult)
+        tt(c32("HIT"), c32("BEST"), c32("ST", 1), A.is_lt)
+        ts(c32("MI"), c32("B8"), 7, A.bitwise_and)
+        tt(c32("MTT"), c32("MI"), c32("STR"), A.mult)
+        tt(c32("HD"), c32("MTT"), c32("CA"), A.add)
+        ts(c32("DNI"), c32("HD"), 1023, A.bitwise_and)
+        ts(c32("DNH"), c32("DNI"), float(H), A.add)
+        for k, (o, w, x) in enumerate(to_rows("P5", "KQ1", c32("DNH"))):
+            mm(o, w, x, False, k == 15)
+        act(R("PAY", 0, 512), R("P5", 0, 512))
+        emit("V", lambda: g.vector.tensor_tensor_scan(ap(c32("INC")), ap(R("ONE", 0, 32)), ap(c32("HIT")), 0.0, A.mult, A.add),
+             [R("ONE", 0, 32), c32("HIT")], [c32("INC")])
+        mm(R("P6", 0, 32), a128("LT"), c32("HIT"), True, False)
+        mm(R("P6", 0, 32), a128("BD"), c32("INC"), False, True)
+        ts(c32("CT"), c32("P6"), -383.0, A.is_lt)
+        tt(c32("RD"), c32("P6"), c32("TM"), A.subtract)
+        tt(c32("RE"), c32("RD"), c32("CT"), A.mult)
+        tt(c32("RF"), c32("RE"), c32("TC"), A.add)
+        cp(c32("SLOT"), c32("RF"))
+        cp(IND(R(SL, 0, 640), c32("SLOT")), R("PAY", 0, 512))
+
+    def send(t):
+        dst = T.cores[(rank + 1) % n_ranks]
+        rid, pid, _ = topo.addr(dst)
+        sl = R("SL%d" % t, 0, 128)
+        sync_for("G", [sl], [])
+        g.remote_dma(T["LAND%d" % t][:, :], ap(sl), T.sem["arr%d" % t], T.sem["snt%d" % t], pid, rid, topo.mask(core, dst))
+
+    def grafts(t):
+        g8 = lambda b: R(b, 0, 8)
+        at = lambda gr, w=128: (w * gr, w * gr + w)
+        mm(R("P6", 0, 16), R("SL%d" % t, 0, 128), R("SELC", 0, 16), True, True)
+        cp(R("XI", 0, 16), R("P6", 0, 16))
+        ts(R("XS", 0, 16), R("XI", 0, 16), 8, A.arith_shift_right)
+        cp(R("XF", 0, 16), R("XS", 0, 16))
+        for gr in range(8):
+            if gr > 2:
+                act(R("DG", *at(gr)), a128("IB"), scale=R("XF", gr, gr + 1))
+            else:
+                ts(R("DG", *at(gr)), a128("IB"), R("XF", gr, gr + 1), A.mult)
+            mm(R("P%d" % (gr // 4), *at(gr % 4)), a128("TRI"), R("DG", *at(gr)), True, True)
+        ts(g8("XN"), g8("XF"), 0.0, A.is_lt)
+        ts(g8("DX"), R("XF", 8, 16), 0.0, A.max)
+        tt(g8("XK"), g8("XN"), g8("XF"), A.add)
+        ts(g8("KI"), g8("XK"), 2047.0, A.add)
+        ts(g8("QI"), g8("KI"), 15, A.bitwise_and)
+        ts(g8("CQ"), g8("KI"), 4, A.arith_shift_right)
+        tt(g8("QF"), g8("QI"), g8("G16"), A.add)
+        cp(g8("CF"), g8("CQ"))
+        for gr in range(8):
+            ts(R("QH", *at(gr)), R("IO1", 0, 128), R("QF", gr, gr + 1), A.is_equal)
+        for gr in range(8):
+            ts(R("EQ", *at(gr)), R("P%d" % (gr // 4), *at(gr % 4)), R("XF", gr, gr + 1), A.is_equal)
+            mm(R("P4", gr, gr + 1), R("EQ", *at(gr)), R("ONE", 0, 1), True, True)
+        ts(g8("WIN"), R("P4", 0, 8), 0.0, A.is_equal)
+        tt(g8("DD"), g8("WIN"), g8("DX"), A.mult)
+        for gr in range(8):
+            ts(R("CHM", *at(gr, 256)), R("IOC", 0, 256), R("CF", gr, gr + 1), A.is_equal, R("DD", gr, gr + 1), A.mult)
+            mm(R("P5", 0, 256), R("QH", *at(gr)), R("CHM", *at(gr, 256)), gr == 0, gr == 7)
+
+    def new_kids(a, b):
+        c = (64 * a, 64 * b)
+        ts(R("ZU", *c), R("P5", *c), 0.0, A.is_equal)
+        tt(R("ZT", *c), R("WK", *c), R("ZU", *c), A.mult)
+        tt(R("WK", *c), R("ZT", *c), R("P5", *c), A.add)
+        for l in range(a, b):
+            lists(l)
+
+    def receive(t):
+        lib = R("YT", H + 128 * t, H + 128 * t + 128)
+        src = T.cores[(rank - 1) % n_ranks]
+        L = "LAND%d" % t
+        g.vector.wait_ge(T.sem["arr%d" % t], len(topo.engines(src, core)))
+        ts(a128("LF"), a128(L), -700000.0, A.is_lt)
+        cp(a128("LI"), a128(L))
+        tt(a128("LT2"), lib, a128("LF"), A.mult)
+        ts(a128("LY"), a128("LI"), 255, A.bitwise_and)
+        tt(lib, a128("LT2"), a128("LY"), A.add)
+
+    do, dko = newd(), newd()
+
+    def out(lo, hi):
+        src = R("YT", H + lo, H + hi)
+        dma("Y", do, T.yo[:, lo:hi], ap(src), [src], [])
+
+    def kids_out():
+        for l in range(4):
+            for s in range(2):
+                mm(R("P0", 128 * s, 128 * s + 128, 1, 32 * l, 32 * l + 32), R("WF", 128 * s + 32 * l, 128 * s + 32 * l + 32), a128("IH"), True, True)
+        ts(R("KOF", 0, 256), R("P0", 0, 256), 1792.0, A.add)
+        for s in range(2):
+            for gr in range(8):
+                c = R("KOF", 128 * s + 16 * gr, 128 * s + 16 * gr + 16)
+                dma("Y", dko, T.ko[gr:gr + 1, 2048 * s:2048 * s + 2048], ap(c), [c], [])
+
+    load_level(0)
+    lists(0)
+    level(0, False)
+    for l in range(1, 4):
+        load_level(l)
+        lists(l)
+    level(1, False)
+    cp(R("NWB", 0, 128), R("NW", 0, 128))
+    ts(c32("NW3"), c32("NW", 3), 1.0 / 256, A.mult)
+    wf(range(4))
+    level(2, False)
+    for l in range(3):
+        kt(l)
+    tt(c32("LANE"), c32("LI2"), c32("LI0"), A.add)
+    ts(c32("LQ"), c32("LANE"), 1.0 / 512, A.mult)
+    ts(c32("LQ2"), c32("LQ"), 2.0, A.add)
+    ts(a128("BQ2"), R("BQ", 256, 384), 1.0 / 256, A.mult)
+    level(3, False)
+    kt_copy()
+
+    for t in range(2):
+        r0 = step(0, constants_1 if t == 0 else lambda: None)
+        r1 = step(1, lambda: (r0(), constants_2() if t == 0 else None))
+        r2 = step(2, r1)
+        donors(t, r2)
+        send(t)
+        grafts(t)
+        new_kids(0, 1)
+        receive(t)
+        if t == 0:
+            level(0, False, lambda: new_kids(1, 2))
+            level(1, False, lambda: (new_kids(2, 4), wf(range(2))))
+            level(2, False, lambda: wf(range(2, 4)))
+            for l in range(3):
+                kt(l)
+            level(3, False)
+            kt_copy()
+        else:
+            out(0, 1536)
+            level(0, True, lambda: new_kids(1, 2))
+            out(1536, 2048)
+            level(1, True, lambda: (new_kids(2, 4), wf(range(2))))
+            out(2048, 2560)
+            level(2, True, lambda: wf(range(2, 4)))
+            kids_out()
+            out(2560, 3072)
+            level(3, True)
+            out(3072, 3584)
+
+    for s in ["cV", "cS", "cP", "cG"] + ["d%d" % k for k in range(dmas[0])]:
+        wait("G", s, cnt[s])
+    dst = T.cores[(rank + 1) % n_ranks]
+    for t in range(2):
+        g.wait_ge(T.sem["snt%d" % t], len(topo.engines(core, dst)))

@@ -22,16 +22,17 @@ def declare(dtype, text, packed=False):
 
 declare("bfloat16", "YT:3616 YAB:4096 NWB:128 NW3:32 TG:512 WAB0:1536 WAB1:1536 Y2:1024 SB:1024 NY:1024 AB:1024 BP:512 WT:512 MT:512 DF:4096 GV:1024 "
         "YC:512 LF:128 LT2:128 HIT:32 INC:32 EQ:1024 QH:1024 ONE:128 IB:128 NI:128 BD:128 BD1:128 O256:2048 BQ:2048 KQ0:2048 KQ1:2048 KQ2:2048 MQ:2048 "
-        "W1:2048 W2:2048 AQ:2048 BQ2:128 LB:128 LT:128 TRI:128 I5:128 IO1:128 IOC:256 MCI:256 MC:256")
-declare("float16", "KLH:256 MLH:128 WF:256 KTG:512 XH:32 DNH:32 DG:1024 CHM:2048 IH:128")
+        "W1:2048 W2:2048 AQ:2048 BQ2:128 L00:128 L01:128 L10:128 L11:128 UP:128 DN:128 MLB:128 MLT:128 LB:128 LT:128 TRI:128 I5:128 IO1:128 IOC:256 "
+        "MCI:256 MC:256")
+declare("float16", "KLH:256 WF:256 KTG:512 XH:32 DNH:32 DG:1024 CHM:2048")
 declare("uint16", "UL:384 SEL:32 NL:32 KEYU:32 CU:256 SLOT:32")
 declare("int32", "KLD:256 MLD:128 WTI:2")
-declare("float32", "KT:1536 PAY:512 SL0:640 SL1:640 LAND0:128 LAND1:128 KOF:256 WTF:2")
+declare("float32", "KT:1536 PAY:512 SL0:640 SL1:640 LAND0:128 LAND1:128 KLF:256 KLT:256 KOF:256 KOT:256 WTF:2")
 declare("float32", "WK:256 NW:128 NKB:128 ES:64 TOB:32 DK:32 QC:32 Q0:32 Q1:32 S1:32 S2:32 S3:32 CHI:32 ST:64 NS:64 DS:64 LV:64 NB:32 XG:32 US:64 B1:128 B2:64 "
         "B3:64 BEST:32 CT:32 RD:32 RE:32 RF:32 XF:16 DX:8 XN:8 XK:8 QF:8 CF:8 WIN:8 DD:8 ZU:256 ZT:256 STR:32 SR2:64 SR4:128 SELC:16 LANE:32 LQ:32 LQ2:32 "
-        "TC:32 TM:32 G16:8", True)
+        "TC:32 TM:32 XC:8 NX:8 G16:8", True)
 declare("int32", "LI:128 LY:128 U1I:32 PRI:32 SHI:32 UMI:32 CA:256 CI:256 B8:32 MI:32 MTT:32 HD:32 DNI:32 XI:16 XS:16 KI:8 QI:8 CQ:8 KPI:32 KAI:32 KBI:32 "
-        "LI0:32 LI1:32 LI2:32", True)
+        "XI1:32 LI0:32 LI1:32 LI2:32", True)
 for _k in range(8):
     SCRATCH["P%d" % _k] = ("psum", [128, 512], "float32")
 
@@ -156,6 +157,9 @@ def rank_program(g, core, T, topo):
     def ms(out, v):
         emit("V", lambda: g.vector.memset(ap(out), v), [], [out])
 
+    def vtr(out, a):
+        emit("V", lambda: g.vector.transpose(ap(out), ap(a)), [a], [out])
+
     def act(out, a, func=F.Identity, scale=1.0):
         emit("S", lambda: g.scalar.activation(ap(out), ap(a), func, bias=0.0, scale=num(scale)), rd(a, scale), [out])
 
@@ -182,20 +186,10 @@ def rank_program(g, core, T, topo):
     a128 = lambda b: R(b, 0, 128)
     c32 = lambda b, k=0: R(b, 32 * k, 32 * k + 32)
 
-    dK0, dK1, dM, dL, dT, dW = [newd() for _ in range(6)]
-
-    def load_kids(q, sem, s, l0, l1):
-        for gr in range(8):
-            dst = R("KLD", s * 128 + 16 * gr, s * 128 + 16 * gr + 16, 1, 32 * l0, 32 * l1)
-            dma(q, sem, ap(dst), T.kid[gr:gr + 1, s * 2048 + 512 * l0:s * 2048 + 512 * l1], [], [dst])
-    load_kids("Y", dK0, 0, 0, 1)
-    load_kids("S", dK0, 1, 0, 1)
+    dK, dM, dL, dT, dW = [newd() for _ in range(5)]
+    dma("S", dK, ap(R("KLD", 0, 256)), T.kid[:, :], [], [R("KLD", 0, 256)])
+    dma("Y", dM, ap(R("MLD", 0, 128)), T.mx[:, :], [], [R("MLD", 0, 128)])
     dma("Y", dL, ap(R("YT", H, H + 1536)), T.lv[:, :], [], [R("YT", H, H + 1536)])
-    for gr in range(8):
-        dst = R("MLD", 16 * gr, 16 * gr + 16)
-        dma("S", dM, ap(dst), T.mx[gr:gr + 1, :], [], [dst])
-    load_kids("Y", dK1, 0, 1, 4)
-    load_kids("S", dK1, 1, 1, 4)
     dma("Y", dT, ap(R("TG", 0, 512)), T.tg[:, :], [], [R("TG", 0, 512)])
     dma("Y", dW, ap(R("WTI", 0, 2)), T.wt[:, :], [], [R("WTI", 0, 2)])
 
@@ -204,20 +198,26 @@ def rank_program(g, core, T, topo):
     ms(R("O256", 0, 2048), 256.0)
     ms(R("MQ", 0, 2048), 0.0)
     asel(a128("IB"), a128("ONE"), [[-1, 128]], A.is_equal, 0, 1)
+    iota(R("LI1", 0, 32), [[0, 32]], 1, False)
+    asel(a128("UP"), a128("ONE"), [[1, 128]], A.is_equal, -16, -1)
+    asel(a128("DN"), a128("ONE"), [[1, 128]], A.is_equal, 16, -1)
+    iota(R("LI0", 0, 32), [[16, 32]], 0, False)
     asel(a128("BD1"), a128("ONE"), [[-16, 8], [0, 16]], A.is_ge, 0, 1)
     asel(a128("BD"), a128("BD1"), [[16, 8], [0, 16]], A.is_ge, 15, -1)
-    iota(R("LI0", 0, 32), [[16, 32]], 0, False)
-    iota(R("LI1", 0, 32), [[0, 32]], 1, False)
     asel(R("BQ", 0, 2048), R("O256", 0, 2048), [[-1, 16], [-16, 8], [0, 16]], A.is_equal, 0, 1)
     for k in range(3):
-        asel(R("KQ%d" % k, 0, 2048), R("BQ", 0, 2048), [[0, 16], [0, 8], [1, 16]], A.is_equal, -k, 0)
+        act(R("KQ%d" % k, 0, 2048), R("O256", 0, 2048), scale=0.0)
     asel(a128("LT"), a128("BD"), [[1, 128]], A.is_gt, 0, -1)
     asel(a128("TRI"), a128("ONE"), [[-1, 128]], A.is_gt, 0, 1)
     iota(R("MCI", 0, 256), [[1, 8], [0, 32]], 0, True)
     iota(R("IO1", 0, 128), [[1, 128]], 0, True)
-    iota(R("IOC", 0, 256), [[32, 4], [128, 2], [1, 32]], 0, True)
+    iota(R("IOC", 0, 256), [[1, 256]], 0, True)
     iota(R("G16", 0, 8), [[16, 8]], 0, True)
-    cp(a128("IH"), a128("IB"))
+    ts(c32("XI1"), c32("LI1"), 4, A.arith_shift_right, 1, A.bitwise_and)
+    cp(R("XC", 0, 8), R("XI1", 0, 8))
+    ts(R("NX", 0, 8), R("XC", 0, 8), -1.0, A.mult, 1.0, A.add)
+    for u, v, b in ((0, 0, "IB"), (0, 1, "UP"), (1, 0, "DN"), (1, 1, "IB")):
+        ts(a128("L%d%d" % (u, v)), a128(b), R("XC" if u else "NX", 0, 1), A.mult)
     ts(a128("NI"), a128("IB"), -1.0, A.mult)
     for gr in range(8):
         cp(R("MQ", 16 * gr, 2048, 129), R("BD", 16 * gr, 16 * gr + 16))
@@ -226,6 +226,8 @@ def rank_program(g, core, T, topo):
     ts(c32("Q1"), c32("LI2"), 1.0, A.is_equal, 4096.0, A.mult)
     tt(c32("QC"), c32("Q0"), c32("Q1"), A.add)
     act(R("AQ", 0, 2048), R("MQ", 0, 2048), scale=R("QC", 0, 1))
+    for k in range(3):
+        act(R("KQ%d" % k, k, 2048, 16), R("BQ", k, 2048, 16))
 
     def constants_1():
         cp(R("WTF", 0, 2), R("WTI", 0, 2))
@@ -243,47 +245,51 @@ def rank_program(g, core, T, topo):
         tt(a128("LB"), a128("LB"), a128("IB"), A.add)
         tt(a128("LT"), a128("LB"), a128("I5"), A.add)
 
-    def load_level(l):
-        P = "P%d" % (7 - l)
-        for s in range(2):
-            ts(R("KLH", s * 128, s * 128 + 128, 1, 32 * l, 32 * l + 32), R("KLD", s * 128, s * 128 + 128, 1, 32 * l, 32 * l + 32), -1792.0, A.add)
-        ts(R("MLH", 0, 128, 1, 32 * l, 32 * l + 32), R("MLD", 0, 128, 1, 32 * l, 32 * l + 32), -1.0, A.mult, 1.0, A.add)
-        idr = R("IH", 32 * l, 32 * l + 32, 1, 32 * l, 32 * l + 32)
-        for s in range(2):
-            mm(R(P, 32 * s, 32 * s + 32), R("KLH", s * 128, s * 128 + 128, 1, 32 * l, 32 * l + 32), idr, True, True)
-        mm(R(P, 64, 96), R("MLH", 0, 128, 1, 32 * l, 32 * l + 32), idr, True, True)
-        ts(R("WK", 64 * l, 64 * l + 64), R(P, 0, 64), 1792.0 + H, A.add)
-        cp(c32("NW", l), R(P, 64, 96))
+    def unscramble(P, src, nb):
+        for k in range(nb):
+            for c2 in range(2):
+                for x in range(2):
+                    mm(R(P, 2 * k + c2, 32 * nb, 2 * nb), a128("L%d%d" % (c2, x)), R(src, 32 * k + 16 * x, 32 * k + 16 * x + 16), x == 0, x == 1)
 
-    def lists(l):
-        tt(c32("NKB", l), R("WK", 64 * l + 32, 64 * l + 64), c32("NW", l), A.mult)
-        cp(R("UL", 96 * l + 64, 96 * l + 96), c32("NKB", l))
-        cp(R("UL", 96 * l, 96 * l + 64), R("WK", 64 * l, 64 * l + 64))
+    def load_lists():
+        ts(a128("MLB"), a128("MLD"), -1.0, A.mult, 1.0, A.add)
+        vtr(a128("MLT"), a128("MLB"))
+        unscramble("P6", "MLT", 4)
+        cp(R("NW", 0, 128), R("P6", 0, 128))
+        ts(R("KLF", 0, 256), R("KLD", 0, 256), -1792.0, A.add)
+        vtr(R("KLT", 0, 256), R("KLF", 0, 256))
+        cp(R("KLH", 0, 256), R("KLT", 0, 256))
+        unscramble("P7", "KLH", 8)
+        ts(R("WK", 0, 256), R("P7", 0, 256), 1792.0 + H, A.add)
+
+    def lists():
+        tt(R("NKB", 0, 128), R("WK", 128, 256), R("NW", 0, 128), A.mult)
+        cp(R("UL", 256, 384), R("NKB", 0, 128))
+        cp(R("UL", 0, 256), R("WK", 0, 256))
 
     def level(l, last, between=None):
         W = R("YT", 0, H + 1536 + 512 * l)
         cut = ((0, 8), (8, 32))
+        ul = lambda k, a, b: R("UL", 128 * k + 32 * l + a, 128 * k + 32 * l + b)
         for a, b in cut:
-            act(R("BP", 16 * a, 16 * b), IND(W, R("UL", 96 * l + 64 + a, 96 * l + 64 + b)))
+            act(R("BP", 16 * a, 16 * b), IND(W, ul(2, a, b)))
         if between:
             between()
         for a, b in cut:
             c = (16 * a, 16 * b)
-            tt(R("WT", *c), IND(W, R("UL", 96 * l + a, 96 * l + b)), R("BP", *c), A.add)
-            tt(R("MT", *c), IND(W, R("UL", 96 * l + 32 + a, 96 * l + 32 + b)), R("WT", *c), A.max)
-            o = H + 1536 + 512 * l
-            ts(R("YT", o + c[0], o + c[1]), R("MT", *c), 255.0, A.min)
+            tt(R("WT", *c), IND(W, ul(0, a, b)), R("BP", *c), A.add)
+            tt(R("MT", *c), IND(W, ul(1, a, b)), R("WT", *c), A.max)
+        o = H + 1536 + 512 * l
+        ts(R("YT", o, o + 512), R("MT", 0, 512), 255.0, A.min)
         if not last:
-            act(R("YAB", 2048 + 512 * l, 2560 + 512 * l), IND(W, R("UL", 96 * l + 32, 96 * l + 64)))
+            act(R("YAB", 2048 + 512 * l, 2560 + 512 * l), IND(W, ul(1, 0, 32)))
             if l < 3:
-                act(R("YAB", 512 * l, 512 * l + 512), IND(W, R("UL", 96 * l, 96 * l + 32)))
+                act(R("YAB", 512 * l, 512 * l + 512), IND(W, ul(0, 0, 32)))
             else:
-                cp(R("YAB", 512 * l, 512 * l + 512), IND(W, R("UL", 96 * l, 96 * l + 32)))
+                cp(R("YAB", 512 * l, 512 * l + 512), IND(W, ul(0, 0, 32)))
 
-    def wf(ls):
-        for l in ls:
-            for s in range(2):
-                ts(R("WF", 128 * s + 32 * l, 128 * s + 32 * l + 32), R("WK", 64 * l + 32 * s, 64 * l + 32 * s + 32), -1792.0 - H, A.add)
+    def wf():
+        ts(R("WF", 0, 256), R("WK", 0, 256), -1792.0 - H, A.add)
 
     def kt(l):
         P = "P%d" % (7 - l)
@@ -301,7 +307,7 @@ def rank_program(g, core, T, topo):
         if st == 0:
             D = R("TG", 0, 512)
             y = (R("YAB", 1536, 2048), R("YAB", 3584, 4096))
-            ka, kb = R("WK", 192, 224), R("WK", 224, 256)
+            ka, kb = R("WK", 96, 128), R("WK", 224, 256)
         else:
             D = R(Wc, 1024, 1536)
             y = (R("Y2", 0, 512), R("Y2", 512, 1024))
@@ -310,14 +316,15 @@ def rank_program(g, core, T, topo):
             act(y[0], IND(R("YAB", 0, 1536), c32("NL")))
             ka, kb = c32("KAI"), c32("KBI")
         mm(R("P0", 0, 512), a128("IB"), D, True, True)
-        for s in range(2):
-            mm(R("P%d" % (2 + s), 0, 512), a128("IB"), D, True, False)
+        mm(R("P2", 0, 512), a128("IB"), D, True, False)
         if st == 0:
             for o, w, x in to_rows("P1", "BQ", c32("NW3")):
                 mm(o, w, x, True, True)
             ts(c32("NB"), c32("LANE"), 1536.0, A.add)
         else:
             mm(R("P1", 0, 512), a128("BQ2"), R("KTG", 0, 512), True, True)
+        mm(R("P3", 0, 512), a128("IB"), D, True, False)
+        if st:
             phases("P7", 0, 32, "AQ", "KTG", 0, True, True)
         parts = ((0, 0, 512, "P4"), (1, 0, 256, "P5"), (1, 256, 512, "P0"))
         for s in range(2):
@@ -325,8 +332,8 @@ def rank_program(g, core, T, topo):
             tt(R("SB", *c), y[1 - s], R("P0", 0, 512), A.is_le)
             tt(R("NY", *c), R("P1", 0, 512), y[1 - s], A.mult)
             mm(R("P%d" % (2 + s), 0, 512), a128("NI"), R("NY", *c), False, True)
-        for s, a, b, P in parts:
-            mm(R(P, 0, b - a), a128("NI"), R(y[s][0], y[s][1] + a, y[s][1] + b), True, False)
+            for s2, a, b, P in (parts[1], parts[0]) if s == 0 else parts[2:]:
+                mm(R(P, 0, b - a), a128("NI"), R(y[s2][0], y[s2][1] + a, y[s2][1] + b), True, False)
         for s, a, b, P in parts:
             c = (512 * s + a, 512 * s + b)
             tt(R(Wc, *c), R("SB", *c), R("P%d" % (2 + s), a, b), A.mult)
@@ -351,13 +358,11 @@ def rank_program(g, core, T, topo):
             tt(c32("S2"), c32("TOB"), c32("DK"), A.mult)
         ts(c32("SEL"), c32("S1"), 512.0, A.mult)
         win = R(Wc, 0, 1024 if st == 0 else 1536)
+        act(R(Wn, 1024, 1280), IND(win, R("SEL", 0, 16)))
         if st < 2:
-            act(R(Wn, 1024, 1536), IND(win, c32("SEL")))
             tt(c32("CHI"), c32("S2"), ka, A.add)
             ts(c32("NL"), c32("CHI"), -1536.0 - H, A.add, 0.0, A.max)
-        else:
-            act(R(Wn, 1024, 1280), IND(win, R("SEL", 0, 16)))
-            cp(R(Wn, 1280, 1536), IND(win, R("SEL", 16, 32)))
+        cp(R(Wn, 1280, 1536), IND(win, R("SEL", 16, 32)))
 
         def rest():
             X = "ST" if st == 0 else "NS"
@@ -503,14 +508,11 @@ def rank_program(g, core, T, topo):
         for gr in range(8):
             ts(R("CHM", *at(gr, 256)), R("IOC", 0, 256), R("CF", gr, gr + 1), A.is_equal, R("DD", gr, gr + 1), A.mult)
             mm(R("P5", 0, 256), R("QH", *at(gr)), R("CHM", *at(gr, 256)), gr == 0, gr == 7)
-
-    def new_kids(a, b):
-        c = (64 * a, 64 * b)
+        c = (0, 256)
         ts(R("ZU", *c), R("P5", *c), 0.0, A.is_equal)
         tt(R("ZT", *c), R("WK", *c), R("ZU", *c), A.mult)
         tt(R("WK", *c), R("ZT", *c), R("P5", *c), A.add)
-        for l in range(a, b):
-            lists(l)
+        lists()
 
     def receive(t):
         lib = R("YT", H + 128 * t, H + 128 * t + 128)
@@ -529,26 +531,23 @@ def rank_program(g, core, T, topo):
         src = R("YT", H + lo, H + hi)
         dma("Y", do, T.yo[:, lo:hi], ap(src), [src], [])
 
-    def kids_out():
-        for l in range(4):
-            for s in range(2):
-                mm(R("P0", 128 * s, 128 * s + 128, 1, 32 * l, 32 * l + 32), R("WF", 128 * s + 32 * l, 128 * s + 32 * l + 32), a128("IH"), True, True)
-        ts(R("KOF", 0, 256), R("P0", 0, 256), 1792.0, A.add)
-        for s in range(2):
-            for gr in range(8):
-                c = R("KOF", 128 * s + 16 * gr, 128 * s + 16 * gr + 16)
-                dma("Y", dko, T.ko[gr:gr + 1, 2048 * s:2048 * s + 2048], ap(c), [c], [])
+    def kids_out_1():
+        for k in range(8):
+            for x in range(2):
+                for c2 in range(2):
+                    mm(R("P0", 32 * k + 16 * x, 32 * k + 16 * x + 16), a128("L%d%d" % (x, c2)), R("WF", 2 * k + c2, 256, 16), c2 == 0, c2 == 1)
 
-    load_level(0)
-    lists(0)
-    level(0, False)
-    for l in range(1, 4):
-        load_level(l)
-        lists(l)
-    level(1, False)
+    def kids_out_2():
+        ts(R("KOF", 0, 256), R("P0", 0, 256), 1792.0, A.add)
+        vtr(R("KOT", 0, 256), R("KOF", 0, 256))
+        dma("Y", dko, T.ko[:, :], ap(R("KOT", 0, 256)), [R("KOT", 0, 256)], [])
+
+    load_lists()
+    lists()
+    level(0, False, wf)
     cp(R("NWB", 0, 128), R("NW", 0, 128))
     ts(c32("NW3"), c32("NW", 3), 1.0 / 256, A.mult)
-    wf(range(4))
+    level(1, False)
     level(2, False)
     for l in range(3):
         kt(l)
@@ -566,24 +565,22 @@ def rank_program(g, core, T, topo):
         donors(t, r2)
         send(t)
         grafts(t)
-        new_kids(0, 1)
         receive(t)
         if t == 0:
-            level(0, False, lambda: new_kids(1, 2))
-            level(1, False, lambda: (new_kids(2, 4), wf(range(2))))
-            level(2, False, lambda: wf(range(2, 4)))
+            level(0, False, wf)
+            level(1, False)
             for l in range(3):
                 kt(l)
+            level(2, False)
             level(3, False)
             kt_copy()
         else:
             out(0, 1536)
-            level(0, True, lambda: new_kids(1, 2))
+            level(0, True, wf)
             out(1536, 2048)
-            level(1, True, lambda: (new_kids(2, 4), wf(range(2))))
+            level(1, True, kids_out_1)
             out(2048, 2560)
-            level(2, True, lambda: wf(range(2, 4)))
-            kids_out()
+            level(2, True, kids_out_2)
             out(2560, 3072)
             level(3, True)
             out(3072, 3584)

@@ -20,17 +20,17 @@ def declare(dtype, text, packed=False):
         SCRATCH["SM" + dtype] = ("sbuf", [128, o], dtype)
 
 
-declare("bfloat16", "YT:3616 YAB:4096 NWB:128 NW3:32 TG:512 WAB0:1536 WAB1:1536 Y2:1024 SB:1024 NY:1024 AB:1024 BP:512 WT:512 MT:512 DF:4096 GV:1024 "
-        "YC:512 LF:128 LT2:128 HIT:32 INC:32 EQ:1024 QH:1024 ONE:128 IB:128 NI:128 BD:128 BD1:128 O256:2048 BQ:2048 KQ0:2048 KQ1:2048 KQ2:2048 MQ:2048 "
-        "W1:2048 W2:2048 AQ:2048 BQ2:128 L00:128 L01:128 L10:128 L11:128 UP:128 DN:128 MLB:128 MLT:128 LB:128 LT:128 TRI:128 I5:128 IO1:128 IOC:256 "
+declare("bfloat16", "YT:3616 YAB:4096 YAP:4096 TG:512 WAB0:1536 WAB1:1536 Y2:1024 Y2P:1024 SB:1024 AB:1024 WT:512 MT:512 DF:4096 GV:1024 "
+        "YC:512 LF:128 LT2:128 HIT:32 INC:32 EQ:1024 QH:1024 QD:1024 ONE:128 IB:128 NI:128 BD:128 BD1:128 O256:2048 BQ:2048 KQ0:2048 KQ1:2048 MQ:2048 "
+        "W1:2048 W2:2048 AQ:2048 L00:128 L01:128 L10:128 L11:128 UP:128 DN:128 MLB:128 MLT:128 LB:128 LT:128 TRI:128 I5:128 IO1:128 IOC:256 "
         "MCI:256 MC:256")
 declare("float16", "KLH:256 WF:256 KTG:512 XH:32 DNH:32 DG:1024 CHM:2048")
-declare("uint16", "UL:384 SEL:32 NL:32 KEYU:32 CU:256 SLOT:32")
+declare("uint16", "UL:512 SEL:32 NL:32 KEYU:32 CU:256 SLOT:32")
 declare("int32", "KLD:256 MLD:128 WTI:2")
 declare("float32", "KT:1536 PAY:512 SL0:640 SL1:640 LAND0:128 LAND1:128 KLF:256 KLT:256 KOF:256 KOT:256 WTF:2")
-declare("float32", "WK:256 NW:128 NKB:128 ES:64 TOB:32 DK:32 QC:32 Q0:32 Q1:32 S1:32 S2:32 S3:32 CHI:32 ST:64 NS:64 DS:64 LV:64 NB:32 XG:32 US:64 B1:128 B2:64 "
+declare("float32", "WK:256 NW:128 NKB:256 ES:64 TOB:32 DK:32 QC:32 Q0:32 Q1:32 S1:32 S2:32 S3:32 CHI:32 ST:64 NS:64 DS:64 LV:64 NB:32 XG:32 US:64 B1:128 B2:64 "
         "B3:64 BEST:32 CT:32 RD:32 RE:32 RF:32 XF:16 DX:8 XN:8 XK:8 QF:8 CF:8 WIN:8 DD:8 ZU:256 ZT:256 STR:32 SR2:64 SR4:128 SELC:16 LANE:32 LQ:32 LQ2:32 "
-        "TC:32 TM:32 XC:8 NX:8 G16:8", True)
+        "TC:32 TM:32 NB0:32 ONEF:8 XC:8 NX:8 G16:8", True)
 declare("int32", "LI:128 LY:128 U1I:32 PRI:32 SHI:32 UMI:32 CA:256 CI:256 B8:32 MI:32 MTT:32 HD:32 DNI:32 XI:16 XS:16 KI:8 QI:8 CQ:8 KPI:32 KAI:32 KBI:32 "
         "XI1:32 LI0:32 LI1:32 LI2:32", True)
 for _k in range(8):
@@ -160,8 +160,8 @@ def rank_program(g, core, T, topo):
     def vtr(out, a):
         emit("V", lambda: g.vector.transpose(ap(out), ap(a)), [a], [out])
 
-    def act(out, a, func=F.Identity, scale=1.0):
-        emit("S", lambda: g.scalar.activation(ap(out), ap(a), func, bias=0.0, scale=num(scale)), rd(a, scale), [out])
+    def act(out, a, func=F.Identity, scale=1.0, bias=0.0):
+        emit("S", lambda: g.scalar.activation(ap(out), ap(a), func, bias=num(bias), scale=num(scale)), rd(a, scale, bias), [out])
 
     def mm(out, lhsT, rhs, start, stop):
         emit("P", lambda: g.tensor.matmul(ap(out), ap(lhsT), ap(rhs), start, stop), [lhsT, rhs], [out])
@@ -196,43 +196,49 @@ def rank_program(g, core, T, topo):
     ms(a128("ONE"), 1.0)
     ms(R("YT", 0, H), 0.0)
     ms(R("O256", 0, 2048), 256.0)
-    ms(R("MQ", 0, 2048), 0.0)
     asel(a128("IB"), a128("ONE"), [[-1, 128]], A.is_equal, 0, 1)
     iota(R("LI1", 0, 32), [[0, 32]], 1, False)
     asel(a128("UP"), a128("ONE"), [[1, 128]], A.is_equal, -16, -1)
     asel(a128("DN"), a128("ONE"), [[1, 128]], A.is_equal, 16, -1)
-    iota(R("LI0", 0, 32), [[16, 32]], 0, False)
     asel(a128("BD1"), a128("ONE"), [[-16, 8], [0, 16]], A.is_ge, 0, 1)
     asel(a128("BD"), a128("BD1"), [[16, 8], [0, 16]], A.is_ge, 15, -1)
     asel(R("BQ", 0, 2048), R("O256", 0, 2048), [[-1, 16], [-16, 8], [0, 16]], A.is_equal, 0, 1)
-    for k in range(3):
+    iota(R("LI0", 0, 32), [[16, 32]], 0, False)
+    for k in range(2):
         act(R("KQ%d" % k, 0, 2048), R("O256", 0, 2048), scale=0.0)
     asel(a128("LT"), a128("BD"), [[1, 128]], A.is_gt, 0, -1)
     asel(a128("TRI"), a128("ONE"), [[-1, 128]], A.is_gt, 0, 1)
     iota(R("MCI", 0, 256), [[1, 8], [0, 32]], 0, True)
     iota(R("IO1", 0, 128), [[1, 128]], 0, True)
     iota(R("IOC", 0, 256), [[1, 256]], 0, True)
-    iota(R("G16", 0, 8), [[16, 8]], 0, True)
+    iota(R("G16", 0, 8), [[-16, 8]], 0, True)
     ts(c32("XI1"), c32("LI1"), 4, A.arith_shift_right, 1, A.bitwise_and)
     cp(R("XC", 0, 8), R("XI1", 0, 8))
     ts(R("NX", 0, 8), R("XC", 0, 8), -1.0, A.mult, 1.0, A.add)
     for u, v, b in ((0, 0, "IB"), (0, 1, "UP"), (1, 0, "DN"), (1, 1, "IB")):
         ts(a128("L%d%d" % (u, v)), a128(b), R("XC" if u else "NX", 0, 1), A.mult)
-    ts(a128("NI"), a128("IB"), -1.0, A.mult)
-    for gr in range(8):
-        cp(R("MQ", 16 * gr, 2048, 129), R("BD", 16 * gr, 16 * gr + 16))
-    ts(c32("LI2"), c32("LI1"), 15, A.bitwise_and)
-    ts(c32("Q0"), c32("LI2"), 0.0, A.is_equal)
-    ts(c32("Q1"), c32("LI2"), 1.0, A.is_equal, 4096.0, A.mult)
-    tt(c32("QC"), c32("Q0"), c32("Q1"), A.add)
-    act(R("AQ", 0, 2048), R("MQ", 0, 2048), scale=R("QC", 0, 1))
-    for k in range(3):
-        act(R("KQ%d" % k, k, 2048, 16), R("BQ", k, 2048, 16))
+
+    def constants_0():
+        ts(a128("NI"), a128("IB"), -1.0, A.mult)
+        ms(R("MQ", 0, 2048), 0.0)
+        for gr in range(8):
+            cp(R("MQ", 16 * gr, 2048, 129), R("BD", 16 * gr, 16 * gr + 16))
 
     def constants_1():
+        ts(c32("LI2"), c32("LI1"), 15, A.bitwise_and)
+        ts(c32("Q0"), c32("LI2"), 0.0, A.is_equal)
+        ts(c32("Q1"), c32("LI2"), 1.0, A.is_equal, 4096.0, A.mult)
+        tt(c32("LANE"), c32("LI2"), c32("LI0"), A.add)
+        tt(c32("QC"), c32("Q0"), c32("Q1"), A.add)
+        ts(c32("LQ"), c32("LANE"), 1.0 / 512, A.mult)
+        act(R("AQ", 0, 2048), R("MQ", 0, 2048), scale=R("QC", 0, 1))
+        ts(c32("LQ2"), c32("LQ"), 2.0, A.add)
+        ms(R("ONEF", 0, 8), 1.0)
+        ts(c32("NB0"), c32("LANE"), 1536.0, A.add)
         cp(R("WTF", 0, 2), R("WTI", 0, 2))
-        ts(R("W1", 0, 2048), R("MQ", 0, 2048), R("WTF", 0, 1), A.mult)
-        ts(R("W2", 0, 2048), R("MQ", 0, 2048), R("WTF", 1, 2), A.mult)
+
+    def weighted(k):
+        act(R("W%d" % (k + 1), 0, 2048), R("MQ", 0, 2048), scale=R("WTF", k, k + 1))
 
     def constants_2():
         ts(c32("TC"), c32("LANE"), 128.0, A.add)
@@ -255,96 +261,113 @@ def rank_program(g, core, T, topo):
         ts(a128("MLB"), a128("MLD"), -1.0, A.mult, 1.0, A.add)
         vtr(a128("MLT"), a128("MLB"))
         unscramble("P6", "MLT", 4)
-        cp(R("NW", 0, 128), R("P6", 0, 128))
         ts(R("KLF", 0, 256), R("KLD", 0, 256), -1792.0, A.add)
         vtr(R("KLT", 0, 256), R("KLF", 0, 256))
         cp(R("KLH", 0, 256), R("KLT", 0, 256))
         unscramble("P7", "KLH", 8)
+        constants_0()
+        cp(R("NW", 0, 128), R("P6", 0, 128))
         ts(R("WK", 0, 256), R("P7", 0, 256), 1792.0 + H, A.add)
 
     def lists():
         tt(R("NKB", 0, 128), R("WK", 128, 256), R("NW", 0, 128), A.mult)
-        cp(R("UL", 256, 384), R("NKB", 0, 128))
         cp(R("UL", 0, 256), R("WK", 0, 256))
-
-    def level(l, last, between=None):
-        W = R("YT", 0, H + 1536 + 512 * l)
-        cut = ((0, 8), (8, 32))
-        ul = lambda k, a, b: R("UL", 128 * k + 32 * l + a, 128 * k + 32 * l + b)
-        for a, b in cut:
-            act(R("BP", 16 * a, 16 * b), IND(W, ul(2, a, b)))
-        if between:
-            between()
-        for a, b in cut:
-            c = (16 * a, 16 * b)
-            tt(R("WT", *c), IND(W, ul(0, a, b)), R("BP", *c), A.add)
-            tt(R("MT", *c), IND(W, ul(1, a, b)), R("WT", *c), A.max)
-        o = H + 1536 + 512 * l
-        ts(R("YT", o, o + 512), R("MT", 0, 512), 255.0, A.min)
-        if not last:
-            act(R("YAB", 2048 + 512 * l, 2560 + 512 * l), IND(W, ul(1, 0, 32)))
-            if l < 3:
-                act(R("YAB", 512 * l, 512 * l + 512), IND(W, ul(0, 0, 32)))
-            else:
-                cp(R("YAB", 512 * l, 512 * l + 512), IND(W, ul(0, 0, 32)))
+        cp(R("UL", 256, 384), R("NKB", 0, 128))
 
     def wf():
         ts(R("WF", 0, 256), R("WK", 0, 256), -1792.0 - H, A.add)
 
+    def lists_2():
+        tt(R("NKB", 128, 256), R("WK", 0, 128), R("NW", 0, 128), A.mult)
+        wf()
+        cp(R("UL", 384, 512), R("NKB", 128, 256))
+
+    ul = lambda k, l, a=0, b=32: R("UL", 128 * k + 32 * l + a, 128 * k + 32 * l + b)
+    below = lambda l: R("YT", 0, H + 1536 + 512 * l)
+
+    def table(k, l):
+        n, lo, which = (("YAB", 0, 0), ("YAB", 2048, 1), ("YAP", 0, 3))["abp".index(k)]
+        act(R(n, lo + 512 * l, lo + 512 * l + 512), IND(below(l), ul(which, l)))
+
+    def level(l, tables="", between=None):
+        W = below(l)
+        cut = ((0, 8), (8, 32))
+        bp = lambda a, b: R("YAP", 2048 + 512 * l + 16 * a, 2048 + 512 * l + 16 * b)
+        cp(bp(*cut[0]), IND(W, ul(2, l, *cut[0])))
+        act(bp(*cut[1]), IND(W, ul(2, l, *cut[1])))
+        for k in tables.split():
+            table(k[0], int(k[1]))
+        if between:
+            between()
+        for a, b in cut:
+            c = (16 * a, 16 * b)
+            tt(R("WT", *c), IND(W, ul(0, l, a, b)), bp(a, b), A.add)
+            tt(R("MT", *c), IND(W, ul(1, l, a, b)), R("WT", *c), A.max)
+        o = H + 1536 + 512 * l
+        ts(R("YT", o, o + 512), R("MT", 0, 512), 255.0, A.min)
+
+    def levels():
+        level(0, "b0 a0", lists_2)
+        level(1, "p0 b1")
+        for l in (2, 0, 1):
+            kt(l)
+        level(2, "a1 p1")
+        level(3, "b3 p3", lambda: kt_copy(2))
+        cp(R("YAB", 1536, 2048), IND(below(3), ul(0, 3)))
+        for k in "bap":
+            table(k, 2)
+
     def kt(l):
         P = "P%d" % (7 - l)
-        srcs = (R("WF", 32 * l, 32 * l + 32), R("WF", 128 + 32 * l, 160 + 32 * l), c32("NWB", l))
         for q in range(16):
-            for k in range(3):
-                mm(R(P, q, 512, 16), R("KQ%d" % k, 128 * q, 128 * q + 128), srcs[k], k == 0, k == 2)
+            for k in range(2):
+                mm(R(P, q, 512, 16), R("KQ%d" % k, 128 * q, 128 * q + 128), R("WF", 128 * k + 32 * l, 128 * k + 32 * l + 32), k == 0, k == 1)
 
-    def kt_copy():
-        for l in range(3):
-            act(R("KT", 512 * l, 512 * l + 512), R("P%d" % (7 - l), 0, 512), scale=1.0 / 256)
+    def kt_copy(l):
+        ts(R("KT", 512 * l, 512 * l + 512), R("P%d" % (7 - l), 0, 512), 1.0 / 256, A.mult)
 
     def step(st, fill):
         Wc, Wn = "WAB%d" % (st % 2), "WAB%d" % ((st + 1) % 2)
         if st == 0:
             D = R("TG", 0, 512)
             y = (R("YAB", 1536, 2048), R("YAB", 3584, 4096))
+            yn = (R("YAP", 1536, 2048), R("YAP", 3584, 4096))
             ka, kb = R("WK", 96, 128), R("WK", 224, 256)
         else:
             D = R(Wc, 1024, 1536)
             y = (R("Y2", 0, 512), R("Y2", 512, 1024))
+            yn = (R("Y2P", 0, 512), R("Y2P", 512, 1024))
             cp(y[1], IND(R("YAB", 2048, 3584), c32("NL")))
-            act(R("KTG", 0, 512), IND(R("KT", 0, 1536), c32("NL")))
+            act(yn[1], IND(R("YAP", 2048, 3584), c32("NL")))
             act(y[0], IND(R("YAB", 0, 1536), c32("NL")))
+            act(yn[0], IND(R("YAP", 0, 1536), c32("NL")))
+            if st == 1:
+                act(R("KTG", 0, 512), IND(R("KT", 0, 1536), c32("NL")))
             ka, kb = c32("KAI"), c32("KBI")
+        parts = ((0, 0, 512, "P4"), (1, 0, 256, "P5"), (1, 256, 512, "P1"))
         mm(R("P0", 0, 512), a128("IB"), D, True, True)
-        mm(R("P2", 0, 512), a128("IB"), D, True, False)
-        if st == 0:
-            for o, w, x in to_rows("P1", "BQ", c32("NW3")):
-                mm(o, w, x, True, True)
-            ts(c32("NB"), c32("LANE"), 1536.0, A.add)
-        else:
-            mm(R("P1", 0, 512), a128("BQ2"), R("KTG", 0, 512), True, True)
-        mm(R("P3", 0, 512), a128("IB"), D, True, False)
-        if st:
-            phases("P7", 0, 32, "AQ", "KTG", 0, True, True)
-        parts = ((0, 0, 512, "P4"), (1, 0, 256, "P5"), (1, 256, 512, "P0"))
         for s in range(2):
-            c = (512 * s, 512 * s + 512)
-            tt(R("SB", *c), y[1 - s], R("P0", 0, 512), A.is_le)
-            tt(R("NY", *c), R("P1", 0, 512), y[1 - s], A.mult)
-            mm(R("P%d" % (2 + s), 0, 512), a128("NI"), R("NY", *c), False, True)
-            for s2, a, b, P in (parts[1], parts[0]) if s == 0 else parts[2:]:
-                mm(R(P, 0, b - a), a128("NI"), R(y[s2][0], y[s2][1] + a, y[s2][1] + b), True, False)
+            mm(R("P%d" % (2 + s), 0, 512), a128("IB"), D, True, False)
+        mm(R("P2", 0, 512), a128("NI"), yn[1], False, True)
+        for s, a, b, P in parts[1:] + parts[:1]:
+            mm(R(P, 0, b - a), a128("NI"), R(y[s][0], y[s][1] + a, y[s][1] + b), True, False)
+        mm(R("P3", 0, 512), a128("NI"), yn[0], False, True)
+        for s in range(2):
+            tt(R("SB", 512 * s, 512 * s + 512), y[1 - s], R("P0", 0, 512), A.is_le)
         for s, a, b, P in parts:
             c = (512 * s + a, 512 * s + b)
             tt(R(Wc, *c), R("SB", *c), R("P%d" % (2 + s), a, b), A.mult)
             mm(R(P, 0, b - a), a128("IB"), R(Wc, *c), False, True)
             act(R("AB", *c), R(P, 0, b - a), F.Abs)
-        if st:
+        if st == 1:
+            phases("P7", 0, 32, "AQ", "KTG", 0, True, True)
+        fill()
+        if st == 1:
             ts(c32("KPI"), c32("P7"), (1792.0 + H) * 4097.0, A.add)
             ts(c32("KAI"), c32("KPI"), 4095, A.bitwise_and)
             ts(c32("KBI"), c32("KPI"), 12, A.arith_shift_right)
-        tt(c32("DK"), kb, ka, A.subtract)
-        fill()
+        if st < 2:
+            tt(c32("DK"), kb, ka, A.subtract)
         phases("P6", 0, 64, "MQ", "AB", 0, True, True)
         cp(R("ES", 0, 64), R("P6", 0, 64))
         tt(c32("TOB"), c32("ES", 1), c32("ES"), A.is_lt)
@@ -368,7 +391,7 @@ def rank_program(g, core, T, topo):
             X = "ST" if st == 0 else "NS"
             ts(c32("S3"), c32("TOB"), 2048.0, A.mult)
             tt(c32(X, 1), c32("ES", 1), c32("ES"), A.min)
-            tt(c32(X), c32("S3"), c32("NB"), A.add)
+            tt(c32(X), c32("S3"), c32("NB" if st else "NB0"), A.add)
             if st:
                 tt(R("DS", 0, 64), R("NS", 0, 64), R("ST", 0, 64), A.subtract)
                 tt(R("DS", 0, 64), R("DS", 0, 64), R("LV", 0, 64), A.mult)
@@ -449,9 +472,13 @@ def rank_program(g, core, T, topo):
         tt(R("B2", 0, 64), R("B3", 0, 64), R("P3", 0, 64), A.min)
         tt(R("B1", 0, 64), R("B2", 0, 64), R("P3", 64, 128), A.min)
         tt(c32("BEST"), c32("B1"), c32("B1", 1), A.min)
-        ts(c32("B8"), c32("BEST"), 8.0, A.mult)
         tt(c32("HIT"), c32("BEST"), c32("ST", 1), A.is_lt)
+        ts(c32("B8"), c32("BEST"), 8.0, A.mult)
+        emit("V", lambda: g.vector.tensor_tensor_scan(ap(c32("INC")), ap(R("ONE", 0, 32)), ap(c32("HIT")), 0.0, A.mult, A.add),
+             [R("ONE", 0, 32), c32("HIT")], [c32("INC")])
         ts(c32("MI"), c32("B8"), 7, A.bitwise_and)
+        mm(R("P6", 0, 32), a128("LT"), c32("HIT"), True, False)
+        mm(R("P6", 0, 32), a128("BD"), c32("INC"), False, True)
         tt(c32("MTT"), c32("MI"), c32("STR"), A.mult)
         tt(c32("HD"), c32("MTT"), c32("CA"), A.add)
         ts(c32("DNI"), c32("HD"), 1023, A.bitwise_and)
@@ -459,10 +486,6 @@ def rank_program(g, core, T, topo):
         for k, (o, w, x) in enumerate(to_rows("P5", "KQ1", c32("DNH"))):
             mm(o, w, x, False, k == 15)
         act(R("PAY", 0, 512), R("P5", 0, 512))
-        emit("V", lambda: g.vector.tensor_tensor_scan(ap(c32("INC")), ap(R("ONE", 0, 32)), ap(c32("HIT")), 0.0, A.mult, A.add),
-             [R("ONE", 0, 32), c32("HIT")], [c32("INC")])
-        mm(R("P6", 0, 32), a128("LT"), c32("HIT"), True, False)
-        mm(R("P6", 0, 32), a128("BD"), c32("INC"), False, True)
         ts(c32("CT"), c32("P6"), -383.0, A.is_lt)
         tt(c32("RD"), c32("P6"), c32("TM"), A.subtract)
         tt(c32("RE"), c32("RD"), c32("CT"), A.mult)
@@ -496,10 +519,12 @@ def rank_program(g, core, T, topo):
         ts(g8("KI"), g8("XK"), 2047.0, A.add)
         ts(g8("QI"), g8("KI"), 15, A.bitwise_and)
         ts(g8("CQ"), g8("KI"), 4, A.arith_shift_right)
-        tt(g8("QF"), g8("QI"), g8("G16"), A.add)
+        tt(g8("QF"), g8("G16"), g8("QI"), A.subtract)
         cp(g8("CF"), g8("CQ"))
         for gr in range(8):
-            ts(R("QH", *at(gr)), R("IO1", 0, 128), R("QF", gr, gr + 1), A.is_equal)
+            act(R("QD", *at(gr)), R("IO1", 0, 128), F.Abs, bias=R("QF", gr, gr + 1))
+        for h in range(2):
+            act(R("QH", *at(h, 512)), R("QD", *at(h, 512)), F.Relu, scale=-1.0, bias=R("ONEF", 0, 1))
         for gr in range(8):
             ts(R("EQ", *at(gr)), R("P%d" % (gr // 4), *at(gr % 4)), R("XF", gr, gr + 1), A.is_equal)
             mm(R("P4", gr, gr + 1), R("EQ", *at(gr)), R("ONE", 0, 1), True, True)
@@ -544,45 +569,30 @@ def rank_program(g, core, T, topo):
 
     load_lists()
     lists()
-    level(0, False, wf)
-    cp(R("NWB", 0, 128), R("NW", 0, 128))
-    ts(c32("NW3"), c32("NW", 3), 1.0 / 256, A.mult)
-    level(1, False)
-    level(2, False)
-    for l in range(3):
-        kt(l)
-    tt(c32("LANE"), c32("LI2"), c32("LI0"), A.add)
-    ts(c32("LQ"), c32("LANE"), 1.0 / 512, A.mult)
-    ts(c32("LQ2"), c32("LQ"), 2.0, A.add)
-    ts(a128("BQ2"), R("BQ", 256, 384), 1.0 / 256, A.mult)
-    level(3, False)
-    kt_copy()
+    for k in range(2):
+        act(R("KQ%d" % k, k, 2048, 16), R("BQ", k, 2048, 16))
+    levels()
 
     for t in range(2):
-        r0 = step(0, constants_1 if t == 0 else lambda: None)
-        r1 = step(1, lambda: (r0(), constants_2() if t == 0 else None))
-        r2 = step(2, r1)
+        first = t == 0
+        r0 = step(0, lambda: (constants_1() if first else None, kt_copy(0), kt_copy(1)))
+        r1 = step(1, lambda: (r0(), (constants_2(), weighted(0), weighted(1)) if first else None))
+        r2 = step(2, lambda: r1())
         donors(t, r2)
         send(t)
         grafts(t)
         receive(t)
-        if t == 0:
-            level(0, False, wf)
-            level(1, False)
-            for l in range(3):
-                kt(l)
-            level(2, False)
-            level(3, False)
-            kt_copy()
+        if first:
+            levels()
         else:
             out(0, 1536)
-            level(0, True, wf)
+            level(0, "", wf)
             out(1536, 2048)
-            level(1, True, kids_out_1)
+            level(1, "", kids_out_1)
             out(2048, 2560)
-            level(2, True, kids_out_2)
+            level(2, "", kids_out_2)
             out(2560, 3072)
-            level(3, True)
+            level(3)
             out(3072, 3584)
 
     for s in ["cV", "cS", "cP", "cG"] + ["d%d" % k for k in range(dmas[0])]:

from concourse.mybir import AluOpType as A, ActivationFunctionType as F

H = 16
LIB = 1024
SENT = -1048576.0

SCRATCH, PLACE = {}, {}


def declare(dtype, text, packed=False):
    o = 0
    for item in text.split():
        name, w = item.split(":")
        if packed:
            PLACE[name] = ("SM" + dtype, o)
            o += (int(w) + 7) // 8 * 8
        else:
            SCRATCH[name] = ("sbuf", [128, int(w)], dtype)
    if packed:
        SCRATCH["SM" + dtype] = ("sbuf", [128, o], dtype)


declare("bfloat16", "YT:3616 YAB:4096 YAP:4096 TG:512 WAB0:1536 WAB1:1536 Y2:1024 Y2P:1024 SB:1024 AB:1024 WT:512 MT:512 DF:4096 GV:1024 "
        "YC:512 LF:128 LT2:128 HIT:32 INC:32 EQ:1024 QH:1024 QD:1024 ONE:128 IB:128 NI:128 BD:128 BD1:128 O256:2048 BQ:2048 KQ0:2048 KQ1:2048 MQ:2048 "
        "W1:2048 W2:2048 AQ:2048 L00:128 L01:128 L10:128 L11:128 UP:128 DN:128 MLB:128 MLT:128 LB:128 LT:128 TRI:128 I5:128 IO1:128 IOC:256 "
        "MCI:256 MC:256")
declare("float16", "KLH:256 WF:256 KTG:512 XH:32 DNH:32 DG:1024 CHM:2048")
declare("uint16", "UL:512 SEL:32 NL:32 KEYU:32 CU:256 SLOT:32")
declare("int32", "KLD:256 MLD:128 WTI:2")
declare("float32", "KT:1536 PAY:512 SL0:640 SL1:640 LAND0:128 LAND1:128 KLF:256 KLT:256 KOF:256 KOT:256 WTF:2")
declare("float32", "WK:256 NW:128 NKB:256 ES:64 TOB:32 DK:32 QC:32 Q0:32 Q1:32 S1:32 S2:32 S3:32 CHI:32 ST:64 NS:64 DS:64 LV:64 NB:32 XG:32 US:64 B1:128 B2:64 "
        "B3:64 BEST:32 CT:32 RD:32 RE:32 RF:32 XF:16 DX:8 XN:8 XK:8 QF:8 CF:8 WIN:8 DD:8 ZU:256 ZT:256 STR:32 SR2:64 SR4:128 SELC:16 LANE:32 LQ:32 LQ2:32 "
        "TC:32 TM:32 NB0:32 ONEF:8 XC:8 NX:8 G16:8", True)
declare("int32", "LI:128 LY:128 U1I:32 PRI:32 SHI:32 UMI:32 CA:256 CI:256 B8:32 MI:32 MTT:32 HD:32 DNI:32 XI:16 XS:16 KI:8 QI:8 CQ:8 KPI:32 KAI:32 KBI:32 "
        "XI1:32 LI0:32 LI1:32 LI2:32", True)
for _k in range(8):
    SCRATCH["P%d" % _k] = ("psum", [128, 512], "float32")

SEMAPHORES = ["cV", "cS", "cP", "cG", "arr0", "arr1", "snt0", "snt1"] + ["d%d" % k for k in range(16)]


def rank_program(g, core, T, topo):
    rank = T.rank_of(core)
    if rank is None:
        return
    n_ranks = len(T.cores)
    ENG = {"V": g.vector, "S": g.scalar, "P": g.tensor, "G": g, "Y": g.sync}
    cnt = {s: 0 for s in SEMAPHORES}
    seen = {q: {} for q in ENG}
    clocks = {}
    acc = {}
    dmas = [0]

    def ap(r):
        if r[0] == "ind":
            return ap(r[1]).indirect(ap(r[2]))
        b, lo, hi, st, p0, p1 = r
        if b in PLACE:
            b, o = PLACE[b]
            lo, hi = lo + o, hi + o
        return T[b][p0:p1, lo:hi] if st == 1 else T[b][p0:p1, lo:hi:st]

    def R(b, lo, hi, st=1, p0=0, p1=128):
        return (b, lo, hi, st, p0, p1)

    def is_psum(b):
        return b[0] == "P" and len(b) == 2

    def wait(q, sem, n):
        if seen[q].get(sem, 0) >= n:
            return
        ENG[q].wait_ge(T.sem[sem], n)
        s = seen[q]
        for k, v in list(clocks.get((sem, n), {}).items()) + [(sem, n)]:
            s[k] = max(s.get(k, 0), v)

    def sync_for(q, reads, writes):
        need = {}
        for rs, w in ((reads, False), (writes, True)):
            for (b, lo, hi, st, p0, p1) in rs:
                ps = is_psum(b)
                if ps:
                    lo, hi, p0, p1 = 0, 512, 0, 128
                for (q2, sem, n, lo2, hi2, a0, a1, w2) in acc.get(b, ()):
                    if lo2 >= hi or hi2 <= lo or a0 >= p1 or a1 <= p0:
                        continue
                    if ps and q2 == q and (q == "P" or not (w or w2)):
                        continue
                    if not ps and not (w or w2):
                        continue
                    need[sem] = max(need.get(sem, 0), cnt[sem] if sem[0] == "d" else n)
        for sem in sorted(need, key=lambda s: -sum(clocks.get((s, need[s]), {}).values())):
            wait(q, sem, need[sem])

    def note(q, sem, n, reads, writes):
        for rs, w in ((writes, True), (reads, False)):
            for (b, lo, hi, st, p0, p1) in rs:
                if is_psum(b):
                    lo, hi, p0, p1 = 0, 512, 0, 128
                L = acc.setdefault(b, [])
                if w and st == 1:
                    L[:] = [e for e in L if not (lo <= e[3] and e[4] <= hi and p0 <= e[5] and e[6] <= p1)]
                elif not w:
                    L[:] = [e for e in L if not (e[0] == q and not e[7] and lo <= e[3] and e[4] <= hi and p0 <= e[5] and e[6] <= p1)]
                L.append((q, sem, n, lo, hi, p0, p1, w))

    def emit(q, fn, reads, writes):
        sync_for(q, reads, writes)
        sem = "c" + q
        cnt[sem] += 1
        fn().then_inc(T.sem[sem], 1)
        clocks[(sem, cnt[sem])] = dict(seen[q], **{sem: cnt[sem]})
        note(q, sem, cnt[sem], reads, writes)

    def newd():
        dmas[0] += 1
        return "d%d" % (dmas[0] - 1)

    def dma(q, sem, out, in_, reads, writes):
        sync_for(q, reads, writes)
        cnt[sem] += 16
        ENG[q].dma_start(out, in_).then_inc(T.sem[sem], 16)
        c = dict(seen[q])
        for k, v in clocks.get((sem, cnt[sem] - 16), {}).items():
            c[k] = max(c.get(k, 0), v)
        clocks[(sem, cnt[sem])] = c
        note(q, sem, cnt[sem], reads, writes)

    def IND(win, off):
        return ("ind", win, off)

    def rd(*xs):
        r = []
        for x in xs:
            if isinstance(x, tuple):
                r += [x[1], x[2]] if x[0] == "ind" else [x]
        return r

    def num(x):
        return ap(x) if isinstance(x, tuple) else x

    def tt(out, a, b, op):
        emit("V", lambda: g.vector.tensor_tensor(ap(out), ap(a), ap(b), op), rd(a, b), [out])

    def ts(out, a, s1, op0, s2=None, op1=None):
        if op1 is None:
            emit("V", lambda: g.vector.tensor_scalar(ap(out), ap(a), num(s1), None, op0), rd(a, s1), [out])
        else:
            emit("V", lambda: g.vector.tensor_scalar(ap(out), ap(a), num(s1), num(s2), op0, op1), rd(a, s1, s2), [out])

    def cp(out, a):
        if out[0] == "ind":
            emit("V", lambda: g.vector.tensor_copy(ap(out), ap(a)), rd(a) + [out[2]], [out[1]])
        else:
            emit("V", lambda: g.vector.tensor_copy(ap(out), ap(a)), rd(a), [out])

    def ms(out, v):
        emit("V", lambda: g.vector.memset(ap(out), v), [], [out])

    def vtr(out, a):
        emit("V", lambda: g.vector.transpose(ap(out), ap(a)), [a], [out])

    def act(out, a, func=F.Identity, scale=1.0, bias=0.0):
        emit("S", lambda: g.scalar.activation(ap(out), ap(a), func, bias=num(bias), scale=num(scale)), rd(a, scale, bias), [out])

    def mm(out, lhsT, rhs, start, stop):
        emit("P", lambda: g.tensor.matmul(ap(out), ap(lhsT), ap(rhs), start, stop), [lhsT, rhs], [out])

    def iota(out, pat, chm, small):
        if small:
            emit("G", lambda: g.iota(ap(out), pat, 0, chm, allow_small_or_imprecise_dtypes=True), [], [out])
        else:
            emit("G", lambda: g.iota(ap(out), pat, 0, chm), [], [out])

    def asel(out, in_, pat, op, base, chm):
        emit("G", lambda: g.affine_select(ap(out), ap(in_), pat, op, 0.0, base, chm), [in_], [out])

    def phases(out_b, lo, n, W, src, s0, first, last):
        for q in range(16):
            mm(R(out_b, lo, lo + n), R(W, 128 * q, 128 * q + 128), R(src, s0 + q, s0 + 16 * n, 16), first and q == 0, last and q == 15)

    def to_rows(P, W, src):
        for q in range(16):
            yield R(P, q, 512, 16), R(W, 128 * q, 128 * q + 128), src

    a128 = lambda b: R(b, 0, 128)
    c32 = lambda b, k=0: R(b, 32 * k, 32 * k + 32)

    dK, dM, dL, dT, dW = [newd() for _ in range(5)]
    dma("S", dK, ap(R("KLD", 0, 256)), T.kid[:, :], [], [R("KLD", 0, 256)])
    dma("Y", dM, ap(R("MLD", 0, 128)), T.mx[:, :], [], [R("MLD", 0, 128)])
    dma("Y", dL, ap(R("YT", H, H + 1536)), T.lv[:, :], [], [R("YT", H, H + 1536)])
    dma("Y", dT, ap(R("TG", 0, 512)), T.tg[:, :], [], [R("TG", 0, 512)])
    dma("Y", dW, ap(R("WTI", 0, 2)), T.wt[:, :], [], [R("WTI", 0, 2)])

    ms(a128("ONE"), 1.0)
    ms(R("YT", 0, H), 0.0)
    ms(R("O256", 0, 2048), 256.0)
    asel(a128("IB"), a128("ONE"), [[-1, 128]], A.is_equal, 0, 1)
    iota(R("LI1", 0, 32), [[0, 32]], 1, False)
    asel(a128("UP"), a128("ONE"), [[1, 128]], A.is_equal, -16, -1)
    asel(a128("DN"), a128("ONE"), [[1, 128]], A.is_equal, 16, -1)
    asel(a128("BD1"), a128("ONE"), [[-16, 8], [0, 16]], A.is_ge, 0, 1)
    asel(a128("BD"), a128("BD1"), [[16, 8], [0, 16]], A.is_ge, 15, -1)
    asel(R("BQ", 0, 2048), R("O256", 0, 2048), [[-1, 16], [-16, 8], [0, 16]], A.is_equal, 0, 1)
    iota(R("LI0", 0, 32), [[16, 32]], 0, False)
    for k in range(2):
        act(R("KQ%d" % k, 0, 2048), R("O256", 0, 2048), scale=0.0)
    asel(a128("LT"), a128("BD"), [[1, 128]], A.is_gt, 0, -1)
    asel(a128("TRI"), a128("ONE"), [[-1, 128]], A.is_gt, 0, 1)
    iota(R("MCI", 0, 256), [[1, 8], [0, 32]], 0, True)
    iota(R("IO1", 0, 128), [[1, 128]], 0, True)
    iota(R("IOC", 0, 256), [[1, 256]], 0, True)
    iota(R("G16", 0, 8), [[-16, 8]], 0, True)
    ts(c32("XI1"), c32("LI1"), 4, A.arith_shift_right, 1, A.bitwise_and)
    cp(R("XC", 0, 8), R("XI1", 0, 8))
    ts(R("NX", 0, 8), R("XC", 0, 8), -1.0, A.mult, 1.0, A.add)
    for u, v, b in ((0, 0, "IB"), (0, 1, "UP"), (1, 0, "DN"), (1, 1, "IB")):
        ts(a128("L%d%d" % (u, v)), a128(b), R("XC" if u else "NX", 0, 1), A.mult)

    def constants_0():
        ts(a128("NI"), a128("IB"), -1.0, A.mult)
        ms(R("MQ", 0, 2048), 0.0)
        for gr in range(8):
            cp(R("MQ", 16 * gr, 2048, 129), R("BD", 16 * gr, 16 * gr + 16))

    def constants_1():
        ts(c32("LI2"), c32("LI1"), 15, A.bitwise_and)
        ts(c32("Q0"), c32("LI2"), 0.0, A.is_equal)
        ts(c32("Q1"), c32("LI2"), 1.0, A.is_equal, 4096.0, A.mult)
        tt(c32("LANE"), c32("LI2"), c32("LI0"), A.add)
        tt(c32("QC"), c32("Q0"), c32("Q1"), A.add)
        ts(c32("LQ"), c32("LANE"), 1.0 / 512, A.mult)
        act(R("AQ", 0, 2048), R("MQ", 0, 2048), scale=R("QC", 0, 1))
        ts(c32("LQ2"), c32("LQ"), 2.0, A.add)
        ms(R("ONEF", 0, 8), 1.0)
        ts(c32("NB0"), c32("LANE"), 1536.0, A.add)
        cp(R("WTF", 0, 2), R("WTI", 0, 2))

    def weighted(k):
        act(R("W%d" % (k + 1), 0, 2048), R("MQ", 0, 2048), scale=R("WTF", k, k + 1))

    def constants_2():
        ts(c32("TC"), c32("LANE"), 128.0, A.add)
        ts(c32("TM"), c32("LANE"), -383.0, A.add)
        ts(R("MC", 0, 256), R("MCI", 0, 256), 0.125, A.mult)
        for s in range(2):
            ts(R("SELC", 8 * s, 8 * s + 8), R("BQ", 128 * s, 128 * s + 128, 16), 1.0 / 256, A.mult)
        ts(a128("I5"), a128("IB"), -512.0, A.mult)
        tt(a128("LB"), a128("LT"), a128("BD"), A.subtract)
        tt(a128("LB"), a128("LB"), a128("IB"), A.add)
        tt(a128("LT"), a128("LB"), a128("I5"), A.add)

    def unscramble(P, src, nb):
        for k in range(nb):
            for c2 in range(2):
                for x in range(2):
                    mm(R(P, 2 * k + c2, 32 * nb, 2 * nb), a128("L%d%d" % (c2, x)), R(src, 32 * k + 16 * x, 32 * k + 16 * x + 16), x == 0, x == 1)

    def load_lists():
        ts(a128("MLB"), a128("MLD"), -1.0, A.mult, 1.0, A.add)
        vtr(a128("MLT"), a128("MLB"))
        unscramble("P6", "MLT", 4)
        ts(R("KLF", 0, 256), R("KLD", 0, 256), -1792.0, A.add)
        vtr(R("KLT", 0, 256), R("KLF", 0, 256))
        cp(R("KLH", 0, 256), R("KLT", 0, 256))
        unscramble("P7", "KLH", 8)
        constants_0()
        cp(R("NW", 0, 128), R("P6", 0, 128))
        ts(R("WK", 0, 256), R("P7", 0, 256), 1792.0 + H, A.add)

    def lists():
        tt(R("NKB", 0, 128), R("WK", 128, 256), R("NW", 0, 128), A.mult)
        cp(R("UL", 0, 256), R("WK", 0, 256))
        cp(R("UL", 256, 384), R("NKB", 0, 128))

    def wf():
        ts(R("WF", 0, 256), R("WK", 0, 256), -1792.0 - H, A.add)

    def lists_2():
        tt(R("NKB", 128, 256), R("WK", 0, 128), R("NW", 0, 128), A.mult)
        wf()
        cp(R("UL", 384, 512), R("NKB", 128, 256))

    ul = lambda k, l, a=0, b=32: R("UL", 128 * k + 32 * l + a, 128 * k + 32 * l + b)
    below = lambda l: R("YT", 0, H + 1536 + 512 * l)

    def table(k, l):
        n, lo, which = (("YAB", 0, 0), ("YAB", 2048, 1), ("YAP", 0, 3))["abp".index(k)]
        act(R(n, lo + 512 * l, lo + 512 * l + 512), IND(below(l), ul(which, l)))

    def level(l, tables="", between=None):
        W = below(l)
        cut = ((0, 8), (8, 32))
        bp = lambda a, b: R("YAP", 2048 + 512 * l + 16 * a, 2048 + 512 * l + 16 * b)
        cp(bp(*cut[0]), IND(W, ul(2, l, *cut[0])))
        act(bp(*cut[1]), IND(W, ul(2, l, *cut[1])))
        for k in tables.split():
            table(k[0], int(k[1]))
        if between:
            between()
        for a, b in cut:
            c = (16 * a, 16 * b)
            tt(R("WT", *c), IND(W, ul(0, l, a, b)), bp(a, b), A.add)
            tt(R("MT", *c), IND(W, ul(1, l, a, b)), R("WT", *c), A.max)
        o = H + 1536 + 512 * l
        ts(R("YT", o, o + 512), R("MT", 0, 512), 255.0, A.min)

    def levels():
        level(0, "b0 a0", lists_2)
        level(1, "p0 b1")
        for l in (2, 0, 1):
            kt(l)
        level(2, "a1 p1")
        level(3, "b3 p3", lambda: kt_copy(2))
        cp(R("YAB", 1536, 2048), IND(below(3), ul(0, 3)))
        for k in "bap":
            table(k, 2)

    def kt(l):
        P = "P%d" % (7 - l)
        for q in range(16):
            for k in range(2):
                mm(R(P, q, 512, 16), R("KQ%d" % k, 128 * q, 128 * q + 128), R("WF", 128 * k + 32 * l, 128 * k + 32 * l + 32), k == 0, k == 1)

    def kt_copy(l):
        ts(R("KT", 512 * l, 512 * l + 512), R("P%d" % (7 - l), 0, 512), 1.0 / 256, A.mult)

    def step(st, fill):
        Wc, Wn = "WAB%d" % (st % 2), "WAB%d" % ((st + 1) % 2)
        if st == 0:
            D = R("TG", 0, 512)
            y = (R("YAB", 1536, 2048), R("YAB", 3584, 4096))
            yn = (R("YAP", 1536, 2048), R("YAP", 3584, 4096))
            ka, kb = R("WK", 96, 128), R("WK", 224, 256)
        else:
            D = R(Wc, 1024, 1536)
            y = (R("Y2", 0, 512), R("Y2", 512, 1024))
            yn = (R("Y2P", 0, 512), R("Y2P", 512, 1024))
            cp(y[1], IND(R("YAB", 2048, 3584), c32("NL")))
            act(yn[1], IND(R("YAP", 2048, 3584), c32("NL")))
            act(y[0], IND(R("YAB", 0, 1536), c32("NL")))
            act(yn[0], IND(R("YAP", 0, 1536), c32("NL")))
            if st == 1:
                act(R("KTG", 0, 512), IND(R("KT", 0, 1536), c32("NL")))
            ka, kb = c32("KAI"), c32("KBI")
        parts = ((0, 0, 512, "P4"), (1, 0, 256, "P5"), (1, 256, 512, "P1"))
        mm(R("P0", 0, 512), a128("IB"), D, True, True)
        for s in range(2):
            mm(R("P%d" % (2 + s), 0, 512), a128("IB"), D, True, False)
        mm(R("P2", 0, 512), a128("NI"), yn[1], False, True)
        for s, a, b, P in parts[1:] + parts[:1]:
            mm(R(P, 0, b - a), a128("NI"), R(y[s][0], y[s][1] + a, y[s][1] + b), True, False)
        mm(R("P3", 0, 512), a128("NI"), yn[0], False, True)
        for s in range(2):
            tt(R("SB", 512 * s, 512 * s + 512), y[1 - s], R("P0", 0, 512), A.is_le)
        for s, a, b, P in parts:
            c = (512 * s + a, 512 * s + b)
            tt(R(Wc, *c), R("SB", *c), R("P%d" % (2 + s), a, b), A.mult)
            mm(R(P, 0, b - a), a128("IB"), R(Wc, *c), False, True)
            act(R("AB", *c), R(P, 0, b - a), F.Abs)
        if st == 1:
            phases("P7", 0, 32, "AQ", "KTG", 0, True, True)
        fill()
        if st == 1:
            ts(c32("KPI"), c32("P7"), (1792.0 + H) * 4097.0, A.add)
            ts(c32("KAI"), c32("KPI"), 4095, A.bitwise_and)
            ts(c32("KBI"), c32("KPI"), 12, A.arith_shift_right)
        if st < 2:
            tt(c32("DK"), kb, ka, A.subtract)
        phases("P6", 0, 64, "MQ", "AB", 0, True, True)
        cp(R("ES", 0, 64), R("P6", 0, 64))
        tt(c32("TOB"), c32("ES", 1), c32("ES"), A.is_lt)
        if st == 0:
            tt(c32("S1"), c32("TOB"), c32("LQ"), A.add)
        else:
            ts(c32("S1"), c32("TOB"), -2.0, A.add)
            tt(c32("S3"), c32("S1"), c32("LV"), A.mult)
            tt(c32("S1"), c32("S3"), c32("LQ2"), A.add)
        if st < 2:
            tt(c32("S2"), c32("TOB"), c32("DK"), A.mult)
        ts(c32("SEL"), c32("S1"), 512.0, A.mult)
        win = R(Wc, 0, 1024 if st == 0 else 1536)
        act(R(Wn, 1024, 1280), IND(win, R("SEL", 0, 16)))
        if st < 2:
            tt(c32("CHI"), c32("S2"), ka, A.add)
            ts(c32("NL"), c32("CHI"), -1536.0 - H, A.add, 0.0, A.max)
        cp(R(Wn, 1280, 1536), IND(win, R("SEL", 16, 32)))

        def rest():
            X = "ST" if st == 0 else "NS"
            ts(c32("S3"), c32("TOB"), 2048.0, A.mult)
            tt(c32(X, 1), c32("ES", 1), c32("ES"), A.min)
            tt(c32(X), c32("S3"), c32("NB" if st else "NB0"), A.add)
            if st:
                tt(R("DS", 0, 64), R("NS", 0, 64), R("ST", 0, 64), A.subtract)
                tt(R("DS", 0, 64), R("DS", 0, 64), R("LV", 0, 64), A.mult)
                tt(R("ST", 0, 64), R("DS", 0, 64), R("ST", 0, 64), A.add)
            if st == 0:
                for k in range(2):
                    ts(c32("LV", k), c32("CHI"), 1536.0 + H, A.is_ge)
            elif st == 1:
                ts(c32("S3"), c32("CHI"), 1536.0 + H, A.is_ge)
                for k in range(2):
                    tt(c32("LV", k), c32("LV", k), c32("S3"), A.mult)
            if st < 2:
                ts(c32("NB"), c32("CHI"), -1536.0 - H, A.add, 0.0, A.max)
        return rest

    def donors(t, rest):
        D = R("WAB1", 1024, 1536)
        SL = "SL%d" % t
        phases("P6", 0, 32, "W1", "WAB1", 1024, True, True)
        phases("P6", 32, 32, "W2", "WAB1", 1024, True, True)
        rest()
        cp(c32("KEYU"), c32("ST"))
        act(R("YC", 0, 512), IND(R("YAB", 0, 4096), c32("KEYU")))
        ts(c32("XG"), c32("ST"), 2048.0, A.is_ge)
        tt(c32("S3"), c32("XG"), c32("ST"), A.add)
        ts(c32("XH"), c32("S3"), -2048.0, A.add)
        ms(R(SL, 0, 128), SENT)
        cp(R("US", 0, 64), R("P6", 0, 64))
        cp(c32("U1I"), c32("US"))
        tt(c32("PRI"), c32("US"), c32("US", 1), A.mult)
        ts(c32("UMI"), c32("U1I"), 127, A.bitwise_and)
        ts(c32("SHI"), c32("PRI"), 5, A.arith_shift_right)
        ts(c32("STR"), c32("UMI"), 2.0, A.mult, 1.0, A.add)
        for k in range(4):
            act(c32("SR4", k), c32("STR"), scale=4.0)
        tt(c32("CA"), c32("SHI"), c32("US", 1), A.add)
        for k in range(2):
            ts(c32("SR2", k), c32("UMI"), 4.0, A.mult, 2.0, A.add)
        tt(c32("CA", 1), c32("CA"), c32("STR"), A.add)
        tt(R("CA", 64, 128), R("CA", 0, 64), R("SR2", 0, 64), A.add)
        ts(R("CI", 0, 128), R("CA", 0, 128), 1023, A.bitwise_and)
        cp(R("CU", 0, 128), R("CI", 0, 128))
        LW = R("YT", H, H + LIB)
        for k, m in enumerate((1, 3)):
            act(R("GV", 512 * k, 512 * k + 512), IND(LW, c32("CU", m)))
            mm(R("P%d" % (4 + 3 * k), 0, 512), a128("IB"), R("GV", 512 * k, 512 * k + 512), True, False)
            mm(R("P%d" % (4 + 3 * k), 0, 512), a128("NI"), D, False, True)
        for h in range(2):
            mm(R("P%d" % (2 + h), 0, 128), a128("IB"), R("MC", 128 * h, 128 * h + 128), True, False)

        def cand(m):
            c = (512 * m, 512 * m + 512)
            if m in (1, 3):
                act(R("DF", *c), R("P4" if m == 1 else "P7", 0, 512), F.Abs)
            else:
                tt(R("DF", *c), IND(LW, c32("CU", m)), D, A.subtract)
                act(R("DF", *c), R("DF", *c), F.Abs)
        cand(0)
        cand(1)
        tt(R("CA", 128, 256), R("CA", 0, 128), R("SR4", 0, 128), A.add)
        cand(2)
        ts(R("CI", 128, 256), R("CA", 128, 256), 1023, A.bitwise_and)
        cp(R("CU", 128, 256), R("CI", 128, 256))
        cand(3)
        phases("P2", 0, 64, "MQ", "DF", 0, False, False)
        phases("P2", 64, 64, "MQ", "DF", 1024, False, True)
        mm(R("P5", 0, 512), a128("IB"), R("YC", 0, 512), True, False)
        for o, w, x in to_rows("P5", "KQ0", c32("XH")):
            mm(o, w, x, False, False)
        cand(4)
        cand(5)
        phases("P3", 0, 64, "MQ", "DF", 2048, False, False)
        cand(6)
        cp(R("B1", 0, 128), R("P2", 0, 128))
        cand(7)
        tt(R("B3", 0, 64), R("B1", 0, 64), R("B1", 64, 128), A.min)
        phases("P3", 64, 64, "MQ", "DF", 3072, False, True)
        tt(R("B2", 0, 64), R("B3", 0, 64), R("P3", 0, 64), A.min)
        tt(R("B1", 0, 64), R("B2", 0, 64), R("P3", 64, 128), A.min)
        tt(c32("BEST"), c32("B1"), c32("B1", 1), A.min)
        tt(c32("HIT"), c32("BEST"), c32("ST", 1), A.is_lt)
        ts(c32("B8"), c32("BEST"), 8.0, A.mult)
        emit("V", lambda: g.vector.tensor_tensor_scan(ap(c32("INC")), ap(R("ONE", 0, 32)), ap(c32("HIT")), 0.0, A.mult, A.add),
             [R("ONE", 0, 32), c32("HIT")], [c32("INC")])
        ts(c32("MI"), c32("B8"), 7, A.bitwise_and)
        mm(R("P6", 0, 32), a128("LT"), c32("HIT"), True, False)
        mm(R("P6", 0, 32), a128("BD"), c32("INC"), False, True)
        tt(c32("MTT"), c32("MI"), c32("STR"), A.mult)
        tt(c32("HD"), c32("MTT"), c32("CA"), A.add)
        ts(c32("DNI"), c32("HD"), 1023, A.bitwise_and)
        ts(c32("DNH"), c32("DNI"), float(H), A.add)
        for k, (o, w, x) in enumerate(to_rows("P5", "KQ1", c32("DNH"))):
            mm(o, w, x, False, k == 15)
        act(R("PAY", 0, 512), R("P5", 0, 512))
        ts(c32("CT"), c32("P6"), -383.0, A.is_lt)
        tt(c32("RD"), c32("P6"), c32("TM"), A.subtract)
        tt(c32("RE"), c32("RD"), c32("CT"), A.mult)
        tt(c32("RF"), c32("RE"), c32("TC"), A.add)
        cp(c32("SLOT"), c32("RF"))
        cp(IND(R(SL, 0, 640), c32("SLOT")), R("PAY", 0, 512))

    def send(t):
        dst = T.cores[(rank + 1) % n_ranks]
        rid, pid, _ = topo.addr(dst)
        sl = R("SL%d" % t, 0, 128)
        sync_for("G", [sl], [])
        g.remote_dma(T["LAND%d" % t][:, :], ap(sl), T.sem["arr%d" % t], T.sem["snt%d" % t], pid, rid, topo.mask(core, dst))

    def grafts(t):
        g8 = lambda b: R(b, 0, 8)
        at = lambda gr, w=128: (w * gr, w * gr + w)
        mm(R("P6", 0, 16), R("SL%d" % t, 0, 128), R("SELC", 0, 16), True, True)
        cp(R("XI", 0, 16), R("P6", 0, 16))
        ts(R("XS", 0, 16), R("XI", 0, 16), 8, A.arith_shift_right)
        cp(R("XF", 0, 16), R("XS", 0, 16))
        for gr in range(8):
            if gr > 2:
                act(R("DG", *at(gr)), a128("IB"), scale=R("XF", gr, gr + 1))
            else:
                ts(R("DG", *at(gr)), a128("IB"), R("XF", gr, gr + 1), A.mult)
            mm(R("P%d" % (gr // 4), *at(gr % 4)), a128("TRI"), R("DG", *at(gr)), True, True)
        ts(g8("XN"), g8("XF"), 0.0, A.is_lt)
        ts(g8("DX"), R("XF", 8, 16), 0.0, A.max)
        tt(g8("XK"), g8("XN"), g8("XF"), A.add)
        ts(g8("KI"), g8("XK"), 2047.0, A.add)
        ts(g8("QI"), g8("KI"), 15, A.bitwise_and)
        ts(g8("CQ"), g8("KI"), 4, A.arith_shift_right)
        tt(g8("QF"), g8("G16"), g8("QI"), A.subtract)
        cp(g8("CF"), g8("CQ"))
        for gr in range(8):
            act(R("QD", *at(gr)), R("IO1", 0, 128), F.Abs, bias=R("QF", gr, gr + 1))
        for h in range(2):
            act(R("QH", *at(h, 512)), R("QD", *at(h, 512)), F.Relu, scale=-1.0, bias=R("ONEF", 0, 1))
        for gr in range(8):
            ts(R("EQ", *at(gr)), R("P%d" % (gr // 4), *at(gr % 4)), R("XF", gr, gr + 1), A.is_equal)
            mm(R("P4", gr, gr + 1), R("EQ", *at(gr)), R("ONE", 0, 1), True, True)
        ts(g8("WIN"), R("P4", 0, 8), 0.0, A.is_equal)
        tt(g8("DD"), g8("WIN"), g8("DX"), A.mult)
        for gr in range(8):
            ts(R("CHM", *at(gr, 256)), R("IOC", 0, 256), R("CF", gr, gr + 1), A.is_equal, R("DD", gr, gr + 1), A.mult)
            mm(R("P5", 0, 256), R("QH", *at(gr)), R("CHM", *at(gr, 256)), gr == 0, gr == 7)
        c = (0, 256)
        ts(R("ZU", *c), R("P5", *c), 0.0, A.is_equal)
        tt(R("ZT", *c), R("WK", *c), R("ZU", *c), A.mult)
        tt(R("WK", *c), R("ZT", *c), R("P5", *c), A.add)
        lists()

    def receive(t):
        lib = R("YT", H + 128 * t, H + 128 * t + 128)
        src = T.cores[(rank - 1) % n_ranks]
        L = "LAND%d" % t
        g.vector.wait_ge(T.sem["arr%d" % t], len(topo.engines(src, core)))
        ts(a128("LF"), a128(L), -700000.0, A.is_lt)
        cp(a128("LI"), a128(L))
        tt(a128("LT2"), lib, a128("LF"), A.mult)
        ts(a128("LY"), a128("LI"), 255, A.bitwise_and)
        tt(lib, a128("LT2"), a128("LY"), A.add)

    do, dko = newd(), newd()

    def out(lo, hi):
        src = R("YT", H + lo, H + hi)
        dma("Y", do, T.yo[:, lo:hi], ap(src), [src], [])

    def kids_out_1():
        for k in range(8):
            for x in range(2):
                for c2 in range(2):
                    mm(R("P0", 32 * k + 16 * x, 32 * k + 16 * x + 16), a128("L%d%d" % (x, c2)), R("WF", 2 * k + c2, 256, 16), c2 == 0, c2 == 1)

    def kids_out_2():
        ts(R("KOF", 0, 256), R("P0", 0, 256), 1792.0, A.add)
        vtr(R("KOT", 0, 256), R("KOF", 0, 256))
        dma("Y", dko, T.ko[:, :], ap(R("KOT", 0, 256)), [R("KOT", 0, 256)], [])

    load_lists()
    lists()
    for k in range(2):
        act(R("KQ%d" % k, k, 2048, 16), R("BQ", k, 2048, 16))
    levels()

    for t in range(2):
        first = t == 0
        r0 = step(0, lambda: (constants_1() if first else None, kt_copy(0), kt_copy(1)))
        r1 = step(1, lambda: (r0(), (constants_2(), weighted(0), weighted(1)) if first else None))
        r2 = step(2, lambda: r1())
        donors(t, r2)
        send(t)
        grafts(t)
        receive(t)
        if first:
            levels()
        else:
            out(0, 1536)
            level(0, "", wf)
            out(1536, 2048)
            level(1, "", kids_out_1)
            out(2048, 2560)
            level(2, "", kids_out_2)
            out(2560, 3072)
            level(3)
            out(3072, 3584)

    for s in ["cV", "cS", "cP", "cG"] + ["d%d" % k for k in range(dmas[0])]:
        wait("G", s, cnt[s])
    dst = T.cores[(rank + 1) % n_ranks]
    for t in range(2):
        g.wait_ge(T.sem["snt%d" % t], len(topo.engines(core, dst)))
